import numpy as np, ml_dtypes
CORES = [3,7,11,15,131,135,139,143]
N = 8
import mx_ref
BF = ml_dtypes.bfloat16
def gcols(t, e):
    v = np.concatenate([t.reshape(8, 16, -1, 4), np.zeros((8, 16, 1, 4), BF)], axis=2)
    return np.ascontiguousarray(np.stack([v[g][:, e[g]] for g in range(8)])).reshape(128, -1)
def tile(rs):
    return np.stack(rs, axis=2).reshape(128, -1).astype(BF)
def pick(q, e):
    c = np.concatenate([q[0].reshape(128, -1, 4), np.zeros((128, 1, 4), np.uint8)], axis=1); s = np.concatenate([q[1], np.ones((16, 1), np.uint8)], axis=1)
    return (np.ascontiguousarray(c[:, e].reshape(128, -1)), np.ascontiguousarray(s[:, e]))
def join(*qs):
    return (np.concatenate([q[0] for q in qs], axis=1), np.concatenate([q[1] for q in qs], axis=1))
def put(q, e, v):
    c, s = q[0].reshape(128, -1, 4).copy(), q[1].copy(); c[:, e] = v[0].reshape(128, -1, 4); s[:, e] = v[1]
    return (c.reshape(128, -1), s)
def pk(c, s):
    return (np.ascontiguousarray(c), mx_ref.live(s))
def emit(q):
    return q[0], q[1]
def packed(v, rng):
    q = [mx_ref.quantize(np.ascontiguousarray(v[r])) for r in range(N)]
    return np.stack([a for a, b in q]), np.stack([mx_ref.plane(b, rng) for a, b in q])
def values_of_codes():
    e, c = np.zeros((128, 128, 4), np.float32), np.zeros((128, 2, 4), np.uint8)
    e[np.arange(128), np.arange(128), 0] = 1
    c[:127, :, 0] = np.arange(256).reshape(2, 128).T[:127]
    return mx_ref.matmul(mx_ref.quantize(e.reshape(128, 512).astype(BF)), (c.reshape(128, 8), np.full((16, 2), 127, np.uint8))).T.reshape(-1).astype(np.float64)
CODE_VALUE, SCALE_VALUE = values_of_codes(), 2.0 ** (np.arange(256) - 127.0)
def decode(q):
    return (CODE_VALUE[q[0]].reshape(16, 8, -1, 4) * SCALE_VALUE[q[1]][:, None, :, None] + 0.0).reshape(128, -1).astype(np.float32)
def f(rng, *shape):
    return mx_ref.flush((rng.standard_normal(shape, dtype=np.float32) * np.exp2(rng.integers(-2, 3, shape[:-1] + (1,)))).astype(BF))
def wide(rng, *shape, cols=0):
    v = rng.standard_normal(shape, dtype=np.float32) * np.exp2(rng.integers(-12, 13, shape)).astype(np.float32)
    if cols: v *= np.repeat(np.exp2(rng.integers(-cols, cols + 1, shape[:-2] + (1, shape[-1] // 4))) * (rng.random(shape[:-2] + (1, shape[-1] // 4)) > 0.0625), 4, axis=-1).astype(np.float32)
    return mx_ref.flush(v.astype(BF))
C, H, M, R = 384, 6, 64, 2
def keys(p):
    b = p.reshape(8, 16, -1)[:, :H] > 0
    return np.sum(b * (1 << np.arange(H))[:, None], axis=1)
def cells(a, key):
    a = a.reshape(8, 16, C, 4)
    c = np.zeros((8, 16, M, 4), np.float32)
    for g in range(8):
        for k in np.unique(key[g]): c[g, :, k] = np.max(a[g][:, key[g] == k], axis=1)
    return c.reshape(128, 4 * M).astype(BF)
def big(v, k):
    v = v.astype(np.float32) * np.float32(k)
    v[np.abs(v) < np.float32(2.0 ** -16)] = 0
    return v.astype(BF)
def weights(rng, k, still=0):
    w = big(f(rng, 128, 2048), k).reshape(128, 4, 128, 4)
    w[:, :, np.arange(128) % 16 < still] = 0
    w = w.reshape(128, 2048)
    c, p = packed(np.stack([w] * N), rng)
    return {"wc": c, "ws": p}
def numbers_of(rng):
    return {"x": big(f(rng, N, 128, 4 * C), 1), "u": np.array(f(rng, N, 128, 512)), "v": np.array(f(rng, N, 128, 512))}
def aim(d, x, key, size):
    u = d["u"].reshape(N, 128, 128, 4)
    for i in range(H):
        x[:, :, i // 4, :, i % 4] = np.where((key >> i) & 1, size, -size)
        for g in range(8):
            u[:, :, 16 * g + i] = 0
            u[:, 16 * g + i // 4, 16 * g + i, i % 4] = 1
def setup_inputs(rng):
    return {**numbers_of(rng), **weights(rng, 1)}
def setup_inputs_ties(rng):
    d = numbers_of(rng)
    d["u"].reshape(N, 8, 16, 128, 4)[:, :, 8:] = 0
    x = d["x"].reshape(N, 8, 16, C, 4)
    e = rng.permutation(N)
    for r in range(N):
        a = x[r][:, :, :1].copy()
        k = rng.permutation(C) % 4
        if r == e[1]: k[:] = 2
        x[r][:, :, k == 0] = 0
        x[r][:, :8, k == 1] = 0
        x[r][:, :, k == 2] = a
    x[e[0]] = 0
    return {**d, "x": x.reshape(N, 128, 4 * C), **weights(rng, 1)}
def setup_inputs_near(rng):
    d = numbers_of(rng)
    x = rng.integers(4, 8, (N, 8, 16, C, 4)) * rng.choice([-0.25, 0.25], (N, 8, 16, C, 4))
    x[:, :, :8] = 0
    s = rng.choice([-1.0, 1.0], (N, 8, C))
    x[:, :, 8, :, 0] = s
    x[:, :, 9, :, 0] = -s
    o = rng.permutation(N)
    a = int(np.argmax(o == 1))
    x[a, :, 8:10, :, 0] = 0
    x[a, :, 7, :, 0] = -s[a] * 2.0 ** -27
    k = np.where(o % 2 == 0, 1.0, 2.0 ** -30).astype(np.float32).astype(BF)
    u = d["u"].reshape(N, 128, 128, 4)
    for i in range(H):
        c = rng.choice([-1.0, 0.0, 1.0, 1.0], (N, 8, C))
        x[:, :, i // 4, :, i % 4] = c * 2.0 ** -23
        x[a, :, i // 4, :, i % 4] = (s[a] + c[a] * 0.125) * 2.0 ** -27
        for g in range(8):
            u[:, :, 16 * g + i] = 0
            u[:, 16 * g + i // 4, 16 * g + i, i % 4] = k
            u[:, 16 * g + 7:16 * g + 10, 16 * g + i, 0] = k[:, None]
    return {**d, "x": x.astype(np.float32).reshape(N, 128, 4 * C).astype(BF), **weights(rng, 1, 10)}
def setup_inputs_huge(rng):
    d = numbers_of(rng)
    key = np.stack([np.stack([rng.permutation(C) % M for g in range(8)]) for r in range(N)])
    sign = np.stack([rng.permutation(M) % 2 * 2.0 - 1.0 for g in range(8)])
    size = rng.integers(8, 17, (N, 8, 16, C, 4))
    size[..., :2] = 16
    x = size * 2.0 ** 26 * sign[np.arange(8)[:, None], key][:, :, None, :, None]
    aim(d, x, key, 2.0 ** 30)
    d["u"] = big(d["u"], 2.0 ** 25)
    return {**d, "x": x.astype(np.float32).reshape(N, 128, 4 * C).astype(BF), **weights(rng, 2.0 ** -3, 2)}
def setup_inputs_crowd(rng):
    d = numbers_of(rng)
    e = rng.permutation(N)
    half = rng.permutation(8) < 4
    nil = rng.permutation(8) < 2
    p = int(e[3]) * (M // N) + M // N - 2
    gone = rng.choice([r for r in range(1, N) if r != e[3]])
    there = np.array([k for k in range(M) if k // (M // N) != gone and k not in (p, p + 1)])
    j = rng.permutation(C)
    key, low = np.zeros((N, 8, C), int), np.zeros((N, 8, C), bool)
    for g in range(8):
        c = rng.permutation(there)
        if nil[g]: c = np.concatenate([[0], c[c != 0]])
        for r in range(N):
            k = np.concatenate([c[:1], rng.choice(c[2:], C - 1)])
            if r == e[1] or r == e[0] and half[g]: k[:] = c[0]
            if r == e[2]: k = np.resize(c, C)
            if r == e[3]: key[r, g, j] = np.concatenate([[p, p + 1, p + 1], rng.permutation(k[:-3])])
            else: key[r, g] = rng.permutation(k)
        low[:, g] = (key[:, g] == c[0]) | (key[:, g] == c[1])
    x = d["x"].astype(np.float32).reshape(N, 8, 16, C, 4)
    x = np.where(low[:, :, None, :, None], -1 - np.abs(x), x)
    a = x[e[1]]
    a[:, 2:, 0, 1] = 0
    a[:, 2:, -1, 2] = 0
    b = x[e[3]]
    b[:, 8:, j[0]] = (1 + rng.random((8, 8, 4))) * np.exp2(rng.integers(-1, 4, (8, 8, 4)))
    b[:, 15, j[0], 3] = -127 * 2.0 ** 10
    b[:, 8:, j[1]] = 1 + rng.random((8, 8, 4))
    b[:, 15, j[1], 3] = -2.0 ** 22
    b[:, 8:, j[2]] = -1 - rng.random((8, 8, 4))
    aim(d, x, key, 1.0)
    a[nil, :, -1] = 0
    return {**d, "x": x.astype(np.float32).reshape(N, 128, 4 * C).astype(BF), **weights(rng, 1, 2)}
def setup_inputs_spread(rng):
    d = setup_inputs(rng)
    d["x"] = big(wide(rng, N, 128, 4 * C, cols=6), 1)
    return d
def check_inputs(d):
    b = []
    for k in ("x", "u", "v"):
        a = np.abs(d[k].astype(np.float32))
        if not (np.isfinite(a).all() and ((a == 0) | (a >= 2.0 ** -30) & (a <= 2.0 ** 30)).all()): b.append("a value of " + k)
    if (d["wc"] != d["wc"][:1]).any(): b.append("wc differs between ranks")
    s = [mx_ref.live(p) for p in d["ws"]]
    if any((p != s[0]).any() for p in s): b.append("ws differs between ranks")
    try:
        a = np.abs(decode(pk(d["wc"][0], d["ws"][0])))
        m = np.max(a.reshape(16, 8, 512, 4), axis=(1, 3))
        good = bool(np.isfinite(a).all() and ((m == 0) | (m >= 2.0 ** -30) & (m <= 2.0 ** 30)).all())
    except Exception:
        good = False
    if not good: b.append("a value of W")
    return b
def reference(x, u, v, wc, ws):
    w = pk(wc[0], ws[0])
    qu = [mx_ref.quantize(u[r]) for r in range(N)]
    now = [x[r] for r in range(N)]
    kl = np.zeros((N, 8 * R, C), np.float32)
    for t in range(R):
        held, key, made = [], [], []
        for r in range(N):
            q = mx_ref.quantize(now[r])
            key.append(keys(mx_ref.matmul(qu[r], q)))
            held.append(decode(q))
            made.append(mx_ref.quantize(cells(held[r], key[r])))
            kl[r, 8 * t:8 * t + 8] = key[r]
        merged = np.max(decode(join(*made)).reshape(128, N, 4 * M), axis=1)
        z = mx_ref.quantize(np.ascontiguousarray(merged.astype(BF)))
        g = tile([np.maximum(mx_ref.matmul(pick(w, np.arange(128 * b, 128 * b + 128)), z), np.float32(0.0)) * np.float32(0.015625) for b in range(4)])
        back = decode(mx_ref.quantize(g)).astype(BF)
        for r in range(N):
            now[r] = ((held[r] + gcols(back, key[r]).astype(np.float32)) * np.float32(0.5)).astype(BF)
    y = np.zeros((N, 128, C), np.float32)
    oc, osc = np.zeros((N, 128, 4 * C), np.uint8), np.zeros((N, 16, C), np.uint8)
    for r in range(N):
        q = mx_ref.quantize(now[r])
        y[r] = mx_ref.matmul(mx_ref.quantize(v[r]), q)
        oc[r], osc[r] = emit(q)
    return {"y": y, "kl": kl, "oc": oc, "osc": osc}

@@ -1,0 +1,410 @@
+from concourse.bass import DstId, RemoteDMATransfer
+from concourse.mybir import dt, AluOpType, AxisListType, ActivationFunctionType
+
+C = 384
+M = 64
+ROUNDS = 2
+MS = 400
+BIG = -1.0e20
+MAGIC = 3072
+CODE, U8, BF, F32, I32, U16 = "float8_e4m3fn_x4", "uint8", "bfloat16", "float32", "int32", "uint16"
+
+SCRATCH = {"ps%d" % _b: ("psum", [128, 512], F32) for _b in range(8)}
+for _n, _w, _d in [
+        ("st0", 4 * C, BF), ("st1", 4 * C, BF), ("st2", 4 * C, BF), ("ut", 512, BF), ("vt", 512, BF),
+        ("qu", 128, CODE), ("su", 128, U8), ("qv", 128, CODE), ("sv", 128, U8), ("qw", 512, CODE), ("sw", 512, U8),
+        ("pidx", 4, I32), ("i3", 4, I32), ("f3", 4, F32), ("row", 24, F32), ("dbl", 16, F32), ("cst", 16, F32),
+        ("keyc", 4, F32), ("spare", 4, F32), ("jc", 24, F32), ("gam", 24, F32),
+        ("zi", 128, BF), ("zt", 520, BF), ("zh", 520, BF), ("ji", 128, BF), ("wt", 1024, BF),
+        ("qe", 512, CODE), ("se", 512, U8), ("qj", 256, CODE), ("sj", 256, U8), ("qk", 256, CODE), ("sk", 256, U8),
+        ("jm", C, BF), ("c1", C, BF), ("c2", C, BF), ("ni", C, BF), ("num", C, BF), ("neg", M, BF),
+        ("bits", 4 * C, BF), ("qb", C, CODE), ("sb", C, U8), ("dh", 4 * C, BF), ("kb", C, BF), ("junk", C, BF),
+        ("bsum", 4, F32), ("pen", C, BF), ("klf", C, F32), ("oh", 4 * C, BF), ("cs", 16 + 4 * C, BF), ("ks", C, BF),
+        ("qi", 24, BF), ("qf", 24, F32), ("qg", 24, F32), ("ql", 24, U16), ("keyl", 24, U16),
+        ("vv", C, BF), ("vtr", C, BF), ("ms", C, BF), ("pb", 24, BF), ("pc", 24, F32), ("pd", 24, F32), ("pl", 24, U16),
+        ("win0", 2 * C, BF), ("win1", 2 * C, BF), ("wtr", 2 * C, BF), ("srcf", 24, F32), ("sl", 24, U16),
+        ("em", 4, F32), ("emd", 4, F32), ("stf", 4, F32), ("enf", 4, F32), ("fl", 4, U16), ("el", 4, U16),
+        ("flag0", 848, BF), ("flag1", 848, BF), ("ds", 4 * C, BF), ("mx", 4 * MS, BF), ("at", 512, BF),
+        ("acc", 8 * 4 * M, BF), ("ztile", 512, BF), ("gtile", 512, BF), ("dg", 4 * M, BF), ("gb", 2 * C, BF),
+        ("yb", C, F32)]:
+    SCRATCH[_n] = ("sbuf", [128, _w], _d)
+for _t in range(ROUNDS + 1):
+    SCRATCH["qx%d" % _t] = ("sbuf", [128, C], CODE)
+    SCRATCH["sx%d" % _t] = ("sbuf", [128, C], U8)
+for _t in range(ROUNDS):
+    for _n, _w in (("a", 5 * M), ("c", 4 * M), ("z", 128), ("h", 128)):
+        SCRATCH["q%s%d" % (_n, _t)] = ("sbuf", [128, _w], CODE)
+        SCRATCH["s%s%d" % (_n, _t)] = ("sbuf", [128, _w], U8)
+
+SEMAPHORES = (["ev", "ea", "ep", "eg", "sent"] + [_n + str(_t) for _n in ("onec", "ones", "twoa", "twob") for _t in range(ROUNDS)]
+              + ["d%d" % i for i in range(18)])
+
+
+def rank_program(g, core, T, topo):
+    rank = T.rank_of(core)
+    if rank is None:
+        return
+    op, act = AluOpType, ActivationFunctionType
+    Q = {"v": g.vector, "a": g.scalar, "p": g.tensor, "g": g, "s": g.sync}
+    count = {"v": 0, "a": 0, "p": 0, "g": 0}
+    waited, top, writer, readers, bank, ndma = {}, {}, {}, {}, {}, [0]
+
+    def wait(q, tok):
+        s, n = tok
+        if waited.get((q, s), 0) < n:
+            Q[q].wait_ge(T.sem[s], n)
+            waited[(q, s)] = n
+
+    def order(q, rd, wr):
+        need = {}
+
+        def add(tok):
+            if tok is not None:
+                need[tok[0]] = max(need.get(tok[0], 0), tok[1])
+        for k in rd:
+            add(writer.get(k))
+        for k in wr:
+            add(writer.get(k))
+            for tok in readers.get(k, []):
+                add(tok)
+        for k in list(rd) + list(wr):
+            if k.startswith("ps"):
+                for e, tok in bank.get(k, {}).items():
+                    if e != q:
+                        add(tok)
+        for s in sorted(need):
+            wait(q, (s, need[s]))
+
+    def note(q, rd, wr, tok):
+        top[tok[0]] = max(top.get(tok[0], 0), tok[1])
+        for k in rd:
+            readers.setdefault(k, []).append(tok)
+        for k in wr:
+            writer[k] = tok
+            readers[k] = []
+        for k in list(rd) + list(wr):
+            if k.startswith("ps"):
+                bank.setdefault(k, {})[q] = tok
+
+    def run(q, rd, wr, call):
+        order(q, rd, wr)
+        count[q] += 1
+        call().then_inc(T.sem["e" + q], 1)
+        note(q, rd, wr, ("e" + q, count[q]))
+
+    def dma(q, rd, wr, out, in_):
+        order(q, rd, wr)
+        s = "d%d" % ndma[0]
+        ndma[0] += 1
+        Q[q].dma_start(out, in_).then_inc(T.sem[s], 16)
+        note(q, rd, wr, (s, 16))
+
+    def ts(rd, wr, out, in0, s1, s2, o0, o1=None):
+        if o1 is None:
+            run("v", rd, wr, lambda: g.vector.tensor_scalar(out, in0, s1, None, o0))
+        else:
+            run("v", rd, wr, lambda: g.vector.tensor_scalar(out, in0, s1, s2, o0, o1))
+
+    def tt(rd, wr, out, a, b, o):
+        run("v", rd, wr, lambda: g.vector.tensor_tensor(out, a, b, o))
+
+    def cp(rd, wr, out, in_):
+        run("v", rd, wr, lambda: g.vector.tensor_copy(out, in_))
+
+    def fill(wr, ap, c):
+        run("v", [], wr, lambda: g.vector.memset(ap, c))
+
+    def scan(rd, wr, out, d0, d1, init, o0, o1):
+        run("v", rd, wr, lambda: g.vector.tensor_tensor_scan(out, d0, d1, init, o0, o1))
+
+    def quant(rd, wr, qo, so, in_):
+        run("v", rd, wr, lambda: g.vector.quantize_mx(qo, so, in_))
+
+    def av(rd, wr, out, in_, func, **kw):
+        run("a", rd, wr, lambda: g.scalar.activation(out, in_, func, **kw))
+
+    def mm(rd, b, n, lq, ls, rq, rs):
+        run("p", rd, ["ps%d" % b], lambda: g.tensor.matmul_mx(T["ps%d" % b][:, 0:n], lq, ls, rq, rs, True, True))
+
+    def iota(wr, out, pat, base, cm, small=True):
+        if small:
+            run("g", [], wr, lambda: g.iota(out, pat, base, cm, allow_small_or_imprecise_dtypes=True))
+        else:
+            run("g", [], wr, lambda: g.iota(out, pat, base, cm))
+
+    def ps(b, a, z):
+        return T["ps%d" % b][:, a:z]
+
+    def unpack(rd, b0, n, rq, rs):
+        for b in range(4):
+            mm(rd + ["qe%d" % b], b0 + b, n, T.qe[:, 128 * b:128 * b + 128], T.se[:, 128 * b:128 * b + 128], rq, rs)
+
+    others = [c for c in T.cores if c != core]
+    sib = [c for c in others if c in topo.cores_of(core)][0]
+    far = [c for c in others if c not in topo.cores_of(core) and topo.die(c) == topo.die(core)]
+    mate = [c for c in far if topo.mates(core, c)][0]
+    across = [c for c in far if topo.same_plane(core, c)][0]
+    fourth = [c for c in far if c != mate and c != across][0]
+    off_mask = topo.mask(core, mate) & topo.mask(core, across) & topo.mask(core, fourth)
+    on_mask = topo.mask(core, sib) & ~off_mask
+    n_off, n_on = bin(off_mask).count("1"), bin(on_mask).count("1")
+
+    def dst(c):
+        rid, pid = topo.addr(c, core)
+        return DstId(rid=rid, pnc=pid)
+
+    h = C // 2
+    dma("s", [], ["st0a"], T.st0[:, 0:4 * h], T.x[:, 0:4 * h])
+    dma("a", [], ["ut"], T.ut[:], T.u[:])
+    dma("s", [], ["st0b"], T.st0[:, 4 * h:4 * C], T.x[:, 4 * h:4 * C])
+    dma("s", [], ["qw"], T.qw[:].bitcast(dt.uint8), T.wc[:])
+    dma("s", [], ["sw"], T.sw[:], T.ws[:])
+    dma("s", [], ["vt"], T.vt[:], T.v[:])
+
+    iota(["pidx"], T.pidx[:, 0:1], [[0, 1]], 0, 1, False)
+    iota(["row"], T.row[:], [[1, 24]], 0, 0)
+    iota(["ji"], T.ji[:], [[1, 8], [0, 16]], 0, 0)
+    iota(["zi"], T.zi[:], [[1, 128]], 0, -1)
+    iota(["jm"], T.jm[:], [[0, 24], [1, 16]], 0, 0)
+    iota(["gam"], T.gam[:], [[0, 12], [16, 2]], 191 - MAGIC, 0)
+
+    fill(["win0"], T.win0[:], 0.0)
+    run("g", ["win0"], ["c2"], lambda: g.affine_select(T.c2[:], T.win0[:, 0:C], [[0, 24], [1, 16]], op.is_gt, -4096.0, 0, 0))
+    iota(["ni"], T.ni[:], [[32, 12], [0, 2], [1, 16]], -192, 0)
+    av(["win0"], ["bitz0"], T.bits[:, 0:2 * C], T.win0[:], act.Copy)
+    av(["win0"], ["bitz1"], T.bits[:, 2 * C:4 * C], T.win0[:], act.Copy)
+    ts(["pidx"], ["i30"], T.i3[:, 0:1], T.pidx[:, 0:1], 15, None, op.bitwise_and)
+    ts(["pidx"], ["i31"], T.i3[:, 1:2], T.pidx[:, 0:1], 4, None, op.arith_shift_right)
+    ts(["pidx"], ["i32"], T.i3[:, 2:3], T.pidx[:, 0:1], 4, 1, op.arith_shift_right, op.bitwise_and)
+    fill(["wtz"], T.wt[:], 0.0)
+    cp(["i30", "i31", "i32"], ["f3"], T.f3[:, 0:3], T.i3[:, 0:3])
+    r, grp, par = T.f3[:, 0:1], T.f3[:, 1:2], T.f3[:, 2:3]
+    fill(["ztz0"], T.zt[:], 0.0)
+    ts(["row", "f3"], ["dbl"], T.dbl[:, 0:15], T.row[:, 0:15], r, 1.0, op.is_lt, op.add)
+    fill(["mxz"], T.mx[:, C:4 * MS:MS], 0.0)
+    run("v", ["dbl"], ["pw"], lambda: g.vector.tensor_reduce(T.cst[:, 0:1], T.dbl[:, 0:15], AxisListType.X, op.mult))
+    ts(["zi", "ztz0"], ["zt"], T.zt[:, 3:515:4], T.zi[:], 0.0, None, op.is_equal)
+    pw, wk, wlo, pwi, r64, sp0, nb, sgb, par16, jb = [T.cst[:, i:i + 1] for i in range(10)]
+    ts(["f3", "pw"], ["wk"], wk, r, 6.0, pw, op.is_lt, op.mult)
+    ts(["f3", "pw"], ["wlo"], wlo, r, 4.0, pw, op.is_lt, op.mult)
+    fill(["neg"], T.neg[:], BIG)
+    ts(["ji", "f3", "wk", "wtz"], ["wt0"], T.wt[:, 0:512:4], T.ji[:], grp, wk, op.is_equal, op.mult)
+    ts(["ji", "f3", "wlo", "wtz"], ["wt1"], T.wt[:, 512:1024:4], T.ji[:], grp, wlo, op.is_equal, op.mult)
+    for b in range(4):
+        quant(["zt"], ["qe%d" % b], T.qe[:, 128 * b:128 * b + 128], T.se[:, 128 * b:128 * b + 128], T.zt[:, 3 - b:515 - b])
+    quant(["wt0", "wt1"], ["qk"], T.qk[:], T.sk[:], T.wt[:])
+    quant(["ut"], ["qu"], T.qu[:], T.su[:], T.ut[:])
+    av(["f3"], ["r64"], r64, r, act.Identity, bias=64.0)
+    av(["f3"], ["sgb"], sgb, r, act.Identity, bias=-0.5)
+    av(["f3"], ["nb"], nb, r, act.Identity, scale=-1024.0)
+    av(["row", "r64"], ["keyc"], T.keyc[:], T.row[:, 0:4], act.Identity, scale=16.0, bias=r64)
+    av(["pw"], ["pwi"], pwi, pw, act.Identity, scale=2.0 ** -15)
+    av(["f3"], ["jb"], jb, r, act.Identity, bias=-float(MAGIC * C // 16))
+    av(["f3"], ["sp0"], sp0, r, act.Identity, scale=4.0, bias=385.0)
+    av(["f3"], ["par16"], par16, par, act.Identity, scale=16.0)
+    av(["row", "jb"], ["jc"], T.jc[:], T.row[:], act.Identity, scale=16.0, bias=jb)
+    av(["row", "sp0"], ["spare"], T.spare[:], T.row[:, 0:4], act.Identity, bias=sp0)
+
+    for t in range(ROUNDS):
+        st, nxt = T["st%d" % t], T["st%d" % (t + 1)]
+        qx, sx = T["qx%d" % t], T["sx%d" % t]
+        qa, sa, qc, sc = T["qa%d" % t], T["sa%d" % t], T["qc%d" % t], T["sc%d" % t]
+        qz, sz, qh, sh = T["qz%d" % t], T["sz%d" % t], T["qh%d" % t], T["sh%d" % t]
+        win, flag = T["win%d" % t], T["flag%d" % t]
+        kx, kw, kf = "qx%d" % t, "win%d" % t, "flag%d" % t
+        new = ["st%d_%d" % (t, b) for b in range(4)]
+        kxa, kxb = kx + "a", kx + "b"
+
+        quant(new if t else ["st0a"], [kxa], qx[:, 0:h], sx[:, 0:h], st[:, 0:4 * h])
+        mm(["qu", kxa], 4, h, T.qu[:], T.su[:], qx[:, 0:h], sx[:, 0:h])
+        quant(new if t else ["st0b"], [kxb], qx[:, h:C], sx[:, h:C], st[:, 4 * h:4 * C])
+        mm(["qu", kxb], 5, h, T.qu[:], T.su[:], qx[:, h:C], sx[:, h:C])
+
+        def own(b):
+            mm([kxa, kxb, "qe%d" % b], b, C, T.qe[:, 128 * b:128 * b + 128], T.se[:, 128 * b:128 * b + 128], qx[:], sx[:])
+
+        def half(b):
+            av(["ps%d" % b], ["dh%d" % b], T.dh[:, C * b:C * b + C], ps(b, 0, C), act.Copy, scale=0.5)
+        own(0)
+        half(0)
+        ts(["ps4", "bitz0"], ["bitsa"], T.bits[:, 0:4 * h:4], ps(4, 0, h), 0.0, None, op.is_gt)
+        ts(["ps5", "bitz1"], ["bitsb"], T.bits[:, 4 * h:4 * C:4], ps(5, 0, h), 0.0, None, op.is_gt)
+        for i, nm in enumerate("ab"):
+            lo, hi = h * i, h * i + h
+            quant(["bits" + nm], ["qb" + nm], T.qb[:, lo:hi], T.sb[:, lo:hi], T.bits[:, 4 * lo:4 * hi])
+            mm(["qk", "qb" + nm], 4 + i, h, T.qk[:, 0:128], T.sk[:, 0:128], T.qb[:, lo:hi], T.sb[:, lo:hi])
+            mm(["qk", "qb" + nm], 6 + i, h, T.qk[:, 0:128], T.sk[:, 0:128], T.qb[:, lo:hi], T.sb[:, lo:hi])
+            av(["ps%d" % (6 + i)], ["kb" + nm], T.kb[:, lo:hi], ps(6 + i, 0, h), act.Identity, bias=64.0)
+        mm(["qk", "qba", "qbb"], 1, C, T.qk[:, 128:256], T.sk[:, 128:256], T.qb[:], T.sb[:])
+        own(2)
+        own(3)
+        av(["ps1", "sgb"], ["junk", "bsum"], T.junk[:], ps(1, 0, C), act.Sign, scale=-1.0, bias=sgb, accum_out=T.bsum[:, 0:1])
+        av(["bsum"], ["cs0"], T.cs[:, 15:16], T.bsum[:, 0:1], act.Copy, scale=0.5)
+        av(["ps1", "nb"], ["pen"], T.pen[:], ps(1, 0, C), act.Abs, scale=1024.0, bias=nb)
+        own(1)
+        if t == 0:
+            av(["ni", "par16"], ["num"], T.num[:], T.ni[:], act.Identity, bias=par16)
+        half(2)
+        half(3)
+        half(1)
+        if t == 0:
+            av(["c2"], ["flag0"], T.flag0[:, 0:C], T.c2[:], act.Relu)
+            av(["c2"], ["atz"], T.at[:, 0:256], T.c2[:, 0:256], act.Relu)
+        kbk = ["kba", "kbb"]
+        av(kbk, ["klf"], T.klf[:], T.kb[:], act.Identity, bias=-64.0)
+        dma("s", ["klf"], [], T.kl[8 * t:8 * t + 8, :], T.klf[0:128:16, :])
+
+        def hot(q):
+            ts(kbk + ["keyc"], ["oh%d" % q], T.oh[:, C * q:C * q + C], T.kb[:], T.keyc[:, q:q + 1], 0.5, op.is_equal, op.mult)
+        ts(["ps4", "f3"], ["oh0a"], T.oh[:, 0:h], ps(4, 0, h), r, 0.5, op.is_equal, op.mult)
+        if t == 0:
+            ts(["jm", "f3"], ["c1"], T.c1[:], T.jm[:], r, 2.0, op.not_equal, op.mult)
+        ts(["ps5", "f3"], ["oh0b"], T.oh[:, h:C], ps(5, 0, h), r, 0.5, op.is_equal, op.mult)
+        scan(["c1"] + kbk, ["ks"], T.ks[:], T.c1[:], T.kb[:], 0.0, op.mult, op.max)
+        hot(1)
+        ts(["ks", "pwi"], ["qi"], T.qi[:], T.ks[:, 15:C:16], pwi, MAGIC - 64 - 7.5, op.mult, op.add)
+        hot(2)
+        ts(["qi"], ["qf"], T.qf[:], T.qi[:], float(C // 16), None, op.mult)
+        hot(3)
+        tt(["qf", "jc"], ["qg"], T.qg[:], T.qf[:], T.jc[:], op.add)
+        scan(["oh0a", "oh0b", "oh1", "oh2", "oh3", "cs0"], ["cs"], T.cs[:, 16:16 + 4 * C], T.oh[:], T.oh[:], T.cs[:, 15:16], op.add, op.add)
+        cp(["qg"], ["ql"], T.ql[:], T.qg[:])
+        ends, starts = T.cs[:, 15 + C:16 + 4 * C:C], T.cs[:, 15:16 + 3 * C:C]
+        tt(["cs", "ql", "pen"], ["vv"], T.vv[:], T.cs[:, 16:16 + 4 * C].indirect(T.ql[:]), T.pen[:], op.subtract)
+        tt(["cs", "cs0"], ["em"], T.em[:], ends, starts, op.is_equal)
+        run("v", ["vv"], ["vtr"], lambda: g.vector.transpose(T.vtr[:], T.vv[:]))
+        tt(["em", "spare"], ["emd"], T.emd[:], T.em[:], T.spare[:], op.mult)
+        scan(["c2", "vtr"], ["ms"], T.ms[:], T.c2[:], T.vtr[:], 0.0, op.add, op.max)
+        tt(["emd", "cs", "cs0"], ["stf"], T.stf[:], T.emd[:], starts, op.add)
+        ts(["ms"], ["pb"], T.pb[:], T.ms[:, 15:C:16], MAGIC + 191 - 7.5, None, op.add)
+        tt(["ms", "gam"], ["pc"], T.pc[:], T.ms[:, 15:C:16], T.gam[:], op.add)
+        tt(["pb", "pc"], ["pd"], T.pd[:], T.pb[:], T.pc[:], op.add)
+        tt(["emd", "cs"], ["enf"], T.enf[:], T.emd[:], ends, op.add)
+        cp(["pd"], ["pl"], T.pl[:], T.pd[:])
+        ts(["stf"], ["fl"], T.fl[:], T.stf[:], 192.0, None, op.add)
+        cp(["pl", "num"], [kw], win[:].indirect(T.pl[:]), T.num[:])
+        run("v", [kw], ["wtr"], lambda: g.vector.transpose(T.wtr[:], win[:]))
+        tt(["wtr"], ["srcf"], T.srcf[:], T.wtr[:, 0:2 * C:32], T.wtr[:, 16:2 * C:32], op.add)
+        ts(["enf"], ["el"], T.el[:], T.enf[:], 191.0, float(C), op.add, op.min)
+        ts(["srcf"], ["sl"], T.sl[:], T.srcf[:], 192.0, None, op.add)
+
+        for b in range(1, 4):
+            av(["dh%d" % b, "sl"], ["ds%d" % b], T.ds[:, C * b:C * b + C], T.dh[:, C * b:C * b + C].indirect(T.sl[:]), act.Copy)
+        cp(["fl", "neg"], [kf], flag[:].indirect(T.fl[:]), T.neg[:])
+        cp(["dh0", "sl"], ["ds0"], T.ds[:, 0:C], T.dh[:, 0:C].indirect(T.sl[:]))
+        for b in (1, 0, 2, 3):
+            scan([kf, "ds%d" % b], ["mx%d" % b], T.mx[:, MS * b:MS * b + C], flag[:, 0:C], T.ds[:, C * b:C * b + C], 0.0, op.add, op.max)
+            if b == 2:
+                ts(["mx0", "mxz", "el"], ["at0"], T.at[:, 256:512:4], T.mx[:, 0:C + 1].indirect(T.el[:]), 2.0, None, op.mult)
+        for b in (1, 2, 3):
+            src = T.mx[:, MS * b:MS * b + C + 1].indirect(T.el[:])
+            out = T.at[:, 256 + b:512:4]
+            if b < 3:
+                av(["mx%d" % b, "mxz", "el"], ["at%d" % b], out, src, act.Copy, scale=2.0)
+            else:
+                ts(["mx%d" % b, "mxz", "el"], ["at%d" % b], out, src, 2.0, None, op.mult)
+        ka = "qa%d" % t
+        quant(["at0", "at1", "at2", "at3", "atz"], [ka], qa[:, 0:128], sa[:, 0:128], T.at[:])
+
+        order("g", [ka], [])
+        for buf, cast, one in ((qa, True, "onec%d" % t), (sa, False, "ones%d" % t)):
+            def vw(a, z):
+                return buf[:, a:z].bitcast(dt.uint8) if cast else buf[:, a:z]
+            g.remote_dma_fused([
+                RemoteDMATransfer(dst_ids=[dst(mate), dst(across)], dma_engine_mask=off_mask, remote_sem=T.sem[one],
+                                  src=vw(M, 2 * M), dsts=[vw(3 * M, 4 * M), vw(4 * M, 5 * M)]),
+                RemoteDMATransfer(dst_ids=[dst(sib)], dma_engine_mask=on_mask, remote_sem=T.sem[one],
+                                  src=vw(M, 2 * M), dst=vw(2 * M, 3 * M)),
+            ], local_sem=T.sem.sent)
+            writer["land1c" if cast else "land1s"] = (one, 2 * n_off + n_on)
+            top[one] = 2 * n_off + n_on
+        top["sent"] = top.get("sent", 0) + 2 * (n_off + n_on)
+
+        ts(["ks", "pwi"], ["keyl"], T.keyl[:], T.ks[:, 15:C:16], pwi, 64.0, op.mult, op.subtract)
+        if t == 0:
+            fill(["ztz"], T.ztile[:, 256:512], 0.0)
+            fill(["gtz"], T.gtile[:, 256:512], 0.0)
+            fill(["win1"], T.win1[:], 0.0)
+            fill(["flag1"], T.flag1[:, 0:C], 0.0)
+            quant(["vt"], ["qv"], T.qv[:], T.sv[:], T.vt[:])
+            ts(["zt"], ["zh"], T.zh[:], T.zt[:], 0.5, None, op.mult)
+            for b in (2, 3):
+                quant(["zh"], ["qj%d" % b], T.qj[:, 128 * b - 256:128 * b - 128], T.sj[:, 128 * b - 256:128 * b - 128], T.zh[:, 3 - b:515 - b])
+
+        twoa, twob = "twoa%d" % t, "twob%d" % t
+        for buf, lnd, cast in ((qa, qc, True), (sa, sc, False)):
+            order("g", ["land1c" if cast else "land1s"], [])
+
+            def vx(bb, a, z):
+                return bb[:, a:z].bitcast(dt.uint8) if cast else bb[:, a:z]
+            g.remote_dma_fused([
+                RemoteDMATransfer(dst_ids=[dst(fourth)], dma_engine_mask=off_mask, remote_sem=T.sem[twob],
+                                  src=vx(buf, M, 3 * M), dst=vx(lnd, 2 * M, 4 * M)),
+                RemoteDMATransfer(dst_ids=[dst(sib)], dma_engine_mask=on_mask, remote_sem=T.sem[twoa],
+                                  src=vx(buf, 3 * M, 5 * M), dst=vx(lnd, 0, 2 * M)),
+            ], local_sem=T.sem.sent)
+        top["sent"] += 2 * (n_off + n_on)
+        writer["land2a"], writer["land2b"] = (twoa, 2 * n_on), (twob, 2 * n_off)
+        top[twoa], top[twob] = 2 * n_on, 2 * n_off
+
+        def slot(i, b):
+            return T.acc[:, (4 * i + b) * M:(4 * i + b + 1) * M]
+
+        def more(i, b0, c0):
+            for b in range(4):
+                out, ko = (slot(i, b), "acc%d_%d" % (i, b)) if i < 7 else (T.ztile[:, b:256:4], "zt_%d" % b)
+                tt(["ps%d" % (b0 + b), "acc%d_%d" % (i - 1, b)], [ko], out, ps(b0 + b, c0, c0 + M), slot(i - 1, b), op.max)
+        unpack([ka, "land1c", "land1s"], 0, 4 * M, qa[:, M:5 * M], sa[:, M:5 * M])
+        for b in range(4):
+            cp(["ps%d" % b], ["acc0_%d" % b], slot(0, b), ps(b, 0, M))
+        for i in range(1, 4):
+            more(i, 0, M * i)
+        unpack(["land2a"], 4, 2 * M, qc[:, 0:2 * M], sc[:, 0:2 * M])
+        more(4, 4, 0)
+        more(5, 4, M)
+        unpack(["land2b"], 0, 2 * M, qc[:, 2 * M:4 * M], sc[:, 2 * M:4 * M])
+        more(6, 0, 0)
+        more(7, 0, M)
+
+        kz, kh = "qz%d" % t, "qh%d" % t
+        quant(["zt_0", "zt_1", "zt_2", "zt_3", "ztz"], [kz], qz[:], sz[:], T.ztile[:])
+        for b in range(4):
+            mm([kz, "qw", "sw"], b, 128, T.qw[:, 128 * b:128 * b + 128], T.sw[:, 128 * b:128 * b + 128], qz[:], sz[:])
+        for b in range(4):
+            out = T.gtile[:, b:256:4]
+            if b % 2 == 0:
+                av(["ps%d" % b], ["gt%d" % b], out, ps(b, 0, M), act.Relu, scale=0.015625)
+            else:
+                ts(["ps%d" % b], ["gt%d" % b], out, ps(b, 0, M), 0.0, 0.015625, op.max, op.mult)
+        quant(["gt0", "gt1", "gt2", "gt3", "gtz"], [kh], qh[:], sh[:], T.gtile[:])
+        unpack([kh], 4, 128, qh[:], sh[:])
+        for b in (2, 3):
+            mm([kxa, kxb, "qj%d" % b], b, C, T.qj[:, 128 * b - 256:128 * b - 128], T.sj[:, 128 * b - 256:128 * b - 128], qx[:], sx[:])
+        ts(["ps4"], ["dg0"], T.dg[:, 0:M], ps(4, 0, M), 0.5, None, op.mult)
+        for b in (1, 2, 3):
+            av(["ps%d" % (4 + b)], ["dg%d" % b], T.dg[:, M * b:M * b + M], ps(4 + b, 0, M), act.Copy, scale=0.5)
+        for b in (2, 3):
+            av(["dg%d" % b, "keyl"], ["gb%d" % b], T.gb[:, C * (b - 2):C * (b - 1)], T.dg[:, M * b:M * b + M].indirect(T.keyl[:]), act.Copy)
+        for b in range(4):
+            ko, out = "st%d_%d" % (t + 1, b), nxt[:, b:4 * C:4]
+            if b < 2:
+                tt(["dg%d" % b, "keyl", "dh%d" % b], [ko], out, T.dg[:, M * b:M * b + M].indirect(T.keyl[:]), T.dh[:, C * b:C * b + C], op.add)
+            else:
+                tt(["ps%d" % b, "gb%d" % b], [ko], out, ps(b, 0, C), T.gb[:, C * (b - 2):C * (b - 1)], op.add)
+
+    qx, sx, st = T["qx%d" % ROUNDS], T["sx%d" % ROUNDS], T["st%d" % ROUNDS]
+    new = ["st%d_%d" % (ROUNDS, b) for b in range(4)]
+    quant(new, ["qfa"], qx[:, 0:h], sx[:, 0:h], st[:, 0:4 * h])
+    mm(["qfa", "qv"], 0, h, T.qv[:], T.sv[:], qx[:, 0:h], sx[:, 0:h])
+    quant(new, ["qfb"], qx[:, h:C], sx[:, h:C], st[:, 4 * h:4 * C])
+    mm(["qfb", "qv"], 1, h, T.qv[:], T.sv[:], qx[:, h:C], sx[:, h:C])
+    av(["ps0"], ["yb0"], T.yb[:, 0:h], ps(0, 0, h), act.Copy)
+    cp(["ps1"], ["yb1"], T.yb[:, h:C], ps(1, 0, h))
+    dma("s", ["qfa", "qfb"], [], T.oc[:], qx[:].bitcast(dt.uint8))
+    dma("a", ["yb0", "yb1"], [], T.y[:], T.yb[:])
+    for k in range(4):
+        dma("s" if k < 3 else "a", ["qfa", "qfb"], [], T.osc[4 * k:4 * k + 4, :], sx[32 * k:32 * k + 4, :])
+
+    for s in sorted(top):
+        if max([n for (q, z), n in waited.items() if z == s] + [0]) < top[s]:
+            wait("g", (s, top[s]))

@@ -7,6 +7,17 @@ ROUNDS = 2
 MS = 400
 BIG = -1.0e20
 MAGIC = 3072
+FOUR = 768
+TINY = 2.0 ** -120
+RUNS = [(0, 128), (128, 256), (256, 384)]
+FL = 2 * C
+SPLIT = 96
+APART = False
+CELL = "aaaa"
+RELU = "vava"
+SQ = "ssag"
+AHEAD = 2
+WIDE = max(hi - lo for lo, hi in RUNS)
 CODE, U8, BF, F32, I32, U16 = "float8_e4m3fn_x4", "uint8", "bfloat16", "float32", "int32", "uint16"
 
 SCRATCH = {"ps%d" % _b: ("psum", [128, 512], F32) for _b in range(8)}
@@ -14,17 +25,18 @@ for _n, _w, _d in [
         ("st0", 4 * C, BF), ("st1", 4 * C, BF), ("st2", 4 * C, BF), ("ut", 512, BF), ("vt", 512, BF),
         ("qu", 128, CODE), ("su", 128, U8), ("qv", 128, CODE), ("sv", 128, U8), ("qw", 512, CODE), ("sw", 512, U8),
         ("pidx", 4, I32), ("i3", 4, I32), ("f3", 4, F32), ("row", 24, F32), ("dbl", 16, F32), ("cst", 16, F32),
-        ("keyc", 4, F32), ("spare", 4, F32), ("jc", 24, F32), ("gam", 24, F32),
-        ("zi", 128, BF), ("zt", 520, BF), ("zh", 520, BF), ("ji", 128, BF), ("wt", 1024, BF),
-        ("qe", 512, CODE), ("se", 512, U8), ("qj", 256, CODE), ("sj", 256, U8), ("qk", 256, CODE), ("sk", 256, U8),
-        ("jm", C, BF), ("c1", C, BF), ("c2", C, BF), ("ni", C, BF), ("num", C, BF), ("neg", M, BF),
+        ("keyc", 4, BF), ("spare", 4, F32), ("jc", 24, F32), ("gam0", 24, F32), ("gam", 24, F32), ("rb", 2, BF),
+        ("zi", 128, BF), ("zt", 520, BF), ("zh", 520, BF), ("ji", 128, BF), ("wt", 512, BF),
+        ("qe", 512, CODE), ("se", 512, U8), ("qj", 512, CODE), ("sj", 512, U8), ("qk", 128, CODE), ("sk", 128, U8),
+        ("jm", WIDE + 16, BF), ("c0", 2 * WIDE, BF), ("c1", C, BF), ("ni", C, BF), ("num", C + M, BF),
         ("bits", 4 * C, BF), ("qb", C, CODE), ("sb", C, U8), ("dh", 4 * C, BF), ("kb", C, BF), ("junk", C, BF),
-        ("bsum", 4, F32), ("pen", C, BF), ("klf", C, F32), ("oh", 4 * C, BF), ("cs", 16 + 4 * C, BF), ("ks", C, BF),
-        ("qi", 24, BF), ("qf", 24, F32), ("qg", 24, F32), ("ql", 24, U16), ("keyl", 24, U16),
-        ("vv", C, BF), ("vtr", C, BF), ("ms", C, BF), ("pb", 24, BF), ("pc", 24, F32), ("pd", 24, F32), ("pl", 24, U16),
-        ("win0", 2 * C, BF), ("win1", 2 * C, BF), ("wtr", 2 * C, BF), ("srcf", 24, F32), ("sl", 24, U16),
-        ("em", 4, F32), ("emd", 4, F32), ("stf", 4, F32), ("enf", 4, F32), ("fl", 4, U16), ("el", 4, U16),
-        ("flag0", 848, BF), ("flag1", 848, BF), ("ds", 4 * C, BF), ("mx", 4 * MS, BF), ("at", 512, BF),
+        ("bsum", 8, F32), ("pen", C, BF), ("pent", C, BF), ("klf", C, F32), ("oh", 4 * C, BF), ("cs", 16 + 4 * C, BF), ("ks", C, BF),
+        ("qi", 24, BF), ("qf", 24, F32), ("qg", 24, F32), ("ql", 24, U16), ("na", 24, F32), ("nb", 24, F32), ("nc", 24, F32),
+        ("keyl", 24, U16), ("kl2", 48, U16),
+        ("vv", C, BF), ("vtr", C, BF), ("ms", C, BF), ("pb", 24, BF), ("pd", 24, F32), ("pl", 28, U16),
+        ("wf0", FL + 848, BF), ("wf1", FL + 848, BF), ("wtr", 2 * C, BF), ("srcf", 24, F32), ("sl", 24, U16),
+        ("em", 4, F32), ("emd", 4, F32), ("stf", 4, F32), ("enf", 4, F32), ("el", 4, U16),
+        ("ds", 4 * C, BF), ("mx", 4 * MS, BF), ("at", 512, BF),
         ("acc", 8 * 4 * M, BF), ("ztile", 512, BF), ("gtile", 512, BF), ("dg", 4 * M, BF), ("gb", 2 * C, BF),
         ("yb", C, F32)]:
     SCRATCH[_n] = ("sbuf", [128, _w], _d)
@@ -36,8 +48,9 @@ for _t in range(ROUNDS):
         SCRATCH["q%s%d" % (_n, _t)] = ("sbuf", [128, _w], CODE)
         SCRATCH["s%s%d" % (_n, _t)] = ("sbuf", [128, _w], U8)
 
-SEMAPHORES = (["ev", "ea", "ep", "eg", "sent"] + [_n + str(_t) for _n in ("onec", "ones", "twoa", "twob") for _t in range(ROUNDS)]
-              + ["d%d" % i for i in range(18)])
+SEMAPHORES = (["ev", "ea", "ep", "eg", "sent"]
+              + [_n + str(_t) for _n in ("sibc", "sibs", "offc", "offs", "fwd", "fth") for _t in range(ROUNDS)]
+              + ["d%d" % i for i in range(24)])
 
 
 def rank_program(g, core, T, topo):
@@ -62,7 +75,7 @@ def rank_program(g, core, T, topo):
             if tok is not None:
                 need[tok[0]] = max(need.get(tok[0], 0), tok[1])
         for k in rd:
-            add(writer.get(k))
+            add(writer[k])
         for k in wr:
             add(writer.get(k))
             for tok in readers.get(k, []):
@@ -135,9 +148,11 @@ def rank_program(g, core, T, topo):
     def ps(b, a, z):
         return T["ps%d" % b][:, a:z]
 
-    def unpack(rd, b0, n, rq, rs):
-        for b in range(4):
-            mm(rd + ["qe%d" % b], b0 + b, n, T.qe[:, 128 * b:128 * b + 128], T.se[:, 128 * b:128 * b + 128], rq, rs)
+    def whole(rd, bk, b, n, rq, rs):
+        mm(rd + ["qe%d" % b], bk, n, T.qe[:, 128 * b:128 * b + 128], T.se[:, 128 * b:128 * b + 128], rq, rs)
+
+    def halved(rd, bk, b, n, rq, rs):
+        mm(rd + ["qj%d" % b], bk, n, T.qj[:, 128 * b:128 * b + 128], T.sj[:, 128 * b:128 * b + 128], rq, rs)
 
     others = [c for c in T.cores if c != core]
     sib = [c for c in others if c in topo.cores_of(core)][0]
@@ -147,263 +162,307 @@ def rank_program(g, core, T, topo):
     fourth = [c for c in far if c != mate and c != across][0]
     off_mask = topo.mask(core, mate) & topo.mask(core, across) & topo.mask(core, fourth)
     on_mask = topo.mask(core, sib) & ~off_mask
-    n_off, n_on = bin(off_mask).count("1"), bin(on_mask).count("1")
 
     def dst(c):
         rid, pid = topo.addr(c, core)
         return DstId(rid=rid, pnc=pid)
 
-    h = C // 2
-    dma("s", [], ["st0a"], T.st0[:, 0:4 * h], T.x[:, 0:4 * h])
+    NR = len(RUNS)
     dma("a", [], ["ut"], T.ut[:], T.u[:])
-    dma("s", [], ["st0b"], T.st0[:, 4 * h:4 * C], T.x[:, 4 * h:4 * C])
-    dma("s", [], ["qw"], T.qw[:].bitcast(dt.uint8), T.wc[:])
+    for i, (lo, hi) in enumerate(RUNS):
+        dma("s", [], ["st0_%d" % i], T.st0[:, 4 * lo:4 * hi], T.x[:, 4 * lo:4 * hi])
+    dma("s", ["st0_%d" % (NR - 1)], ["qw"], T.qw[:].bitcast(dt.uint8), T.wc[:])
     dma("s", [], ["sw"], T.sw[:], T.ws[:])
-    dma("s", [], ["vt"], T.vt[:], T.v[:])
 
-    iota(["pidx"], T.pidx[:, 0:1], [[0, 1]], 0, 1, False)
+    iota(["pidx"], T.pidx[:, 0:1], [[0, 1]], 0, 4, False)
     iota(["row"], T.row[:], [[1, 24]], 0, 0)
     iota(["ji"], T.ji[:], [[1, 8], [0, 16]], 0, 0)
     iota(["zi"], T.zi[:], [[1, 128]], 0, -1)
-    iota(["jm"], T.jm[:], [[0, 24], [1, 16]], 0, 0)
-    iota(["gam"], T.gam[:], [[0, 12], [16, 2]], 191 - MAGIC, 0)
-
-    fill(["win0"], T.win0[:], 0.0)
-    run("g", ["win0"], ["c2"], lambda: g.affine_select(T.c2[:], T.win0[:, 0:C], [[0, 24], [1, 16]], op.is_gt, -4096.0, 0, 0))
+    iota(["jm"], T.jm[:], [[0, WIDE // 16 + 1], [1, 16]], 0, 0)
+    iota(["gam0"], T.gam0[:], [[0, 12], [16, 2]], MAGIC + 183, 0)
     iota(["ni"], T.ni[:], [[32, 12], [0, 2], [1, 16]], -192, 0)
-    av(["win0"], ["bitz0"], T.bits[:, 0:2 * C], T.win0[:], act.Copy)
-    av(["win0"], ["bitz1"], T.bits[:, 2 * C:4 * C], T.win0[:], act.Copy)
-    ts(["pidx"], ["i30"], T.i3[:, 0:1], T.pidx[:, 0:1], 15, None, op.bitwise_and)
-    ts(["pidx"], ["i31"], T.i3[:, 1:2], T.pidx[:, 0:1], 4, None, op.arith_shift_right)
-    ts(["pidx"], ["i32"], T.i3[:, 2:3], T.pidx[:, 0:1], 4, 1, op.arith_shift_right, op.bitwise_and)
+
+    fill(["wf0z"], T.wf0[:, 0:FL], 0.0)
+    dma("g" if "g" in SQ else "s", [], ["vt"], T.vt[:], T.v[:])
+    for i, (lo, hi) in enumerate(RUNS):
+        av(["wf0z"], ["bits%d" % i], T.bits[:, 4 * lo:4 * hi], T.wf0[:, 0:4 * (hi - lo)], act.Copy)
+    ts(["pidx"], ["i30"], T.i3[:, 0:1], T.pidx[:, 0:1], 2, 15, op.arith_shift_right, op.bitwise_and)
+    ts(["pidx"], ["i31"], T.i3[:, 1:2], T.pidx[:, 0:1], 6, None, op.arith_shift_right)
+    ts(["pidx"], ["i32"], T.i3[:, 2:3], T.pidx[:, 0:1], 2, 16, op.arith_shift_right, op.bitwise_and)
+    ts(["pidx"], ["i33"], T.i3[:, 3:4], T.pidx[:, 0:1], 63, None, op.bitwise_and)
     fill(["wtz"], T.wt[:], 0.0)
-    cp(["i30", "i31", "i32"], ["f3"], T.f3[:, 0:3], T.i3[:, 0:3])
-    r, grp, par = T.f3[:, 0:1], T.f3[:, 1:2], T.f3[:, 2:3]
-    fill(["ztz0"], T.zt[:], 0.0)
+    cp(["i30", "i31", "i32", "i33"], ["f3"], T.f3[:], T.i3[:])
+    r, grp, par16, r4 = T.f3[:, 0:1], T.f3[:, 1:2], T.f3[:, 2:3], T.f3[:, 3:4]
+    rb = T.rb[:, 0:1]
+    cp(["i30"], ["rb"], rb, T.i3[:, 0:1])
+    fill(["zhz"], T.zh[:], 0.0)
+    wk, lift, nb, jb, rh, nm = [T.cst[:, i:i + 1] for i in range(6)]
     ts(["row", "f3"], ["dbl"], T.dbl[:, 0:15], T.row[:, 0:15], r, 1.0, op.is_lt, op.add)
-    fill(["mxz"], T.mx[:, C:4 * MS:MS], 0.0)
-    run("v", ["dbl"], ["pw"], lambda: g.vector.tensor_reduce(T.cst[:, 0:1], T.dbl[:, 0:15], AxisListType.X, op.mult))
-    ts(["zi", "ztz0"], ["zt"], T.zt[:, 3:515:4], T.zi[:], 0.0, None, op.is_equal)
-    pw, wk, wlo, pwi, r64, sp0, nb, sgb, par16, jb = [T.cst[:, i:i + 1] for i in range(10)]
-    ts(["f3", "pw"], ["wk"], wk, r, 6.0, pw, op.is_lt, op.mult)
-    ts(["f3", "pw"], ["wlo"], wlo, r, 4.0, pw, op.is_lt, op.mult)
-    fill(["neg"], T.neg[:], BIG)
+    ts(["f3"], ["lt6"], T.dbl[:, 15:16], r, 6.0, 0.5, op.is_lt, op.mult)
+    ts(["f3"], ["lift"], lift, r, 15.0, -64.0, op.is_lt, op.mult)
+    ts(["zi", "zhz"], ["zh"], T.zh[:, 3:515:4], T.zi[:], 0.0, 0.5, op.is_equal, op.mult)
+    run("v", ["dbl", "lt6"], ["wk"], lambda: g.vector.tensor_reduce(wk, T.dbl[:], AxisListType.X, op.mult))
+    ts(["jm", "rb"], ["c0a"], T.c0[:, 0:WIDE], T.jm[:, 16:16 + WIDE], rb, -4096.0, op.is_equal, op.mult)
+    ts(["jm", "rb"], ["c0b"], T.c0[:, WIDE:2 * WIDE], T.jm[:, 15:15 + WIDE], rb, 64.0, op.is_equal, op.mult)
     ts(["ji", "f3", "wk", "wtz"], ["wt0"], T.wt[:, 0:512:4], T.ji[:], grp, wk, op.is_equal, op.mult)
-    ts(["ji", "f3", "wlo", "wtz"], ["wt1"], T.wt[:, 512:1024:4], T.ji[:], grp, wlo, op.is_equal, op.mult)
-    for b in range(4):
-        quant(["zt"], ["qe%d" % b], T.qe[:, 128 * b:128 * b + 128], T.se[:, 128 * b:128 * b + 128], T.zt[:, 3 - b:515 - b])
-    quant(["wt0", "wt1"], ["qk"], T.qk[:], T.sk[:], T.wt[:])
+    tt(["c0a", "c0b"], ["c1"], T.c1[:, 0:WIDE], T.c0[:, 0:WIDE], T.c0[:, WIDE:2 * WIDE], op.add)
+    quant(["wt0"], ["qk"], T.qk[:], T.sk[:], T.wt[:])
     quant(["ut"], ["qu"], T.qu[:], T.su[:], T.ut[:])
-    av(["f3"], ["r64"], r64, r, act.Identity, bias=64.0)
-    av(["f3"], ["sgb"], sgb, r, act.Identity, bias=-0.5)
-    av(["f3"], ["nb"], nb, r, act.Identity, scale=-1024.0)
-    av(["row", "r64"], ["keyc"], T.keyc[:], T.row[:, 0:4], act.Identity, scale=16.0, bias=r64)
-    av(["pw"], ["pwi"], pwi, pw, act.Identity, scale=2.0 ** -15)
-    av(["f3"], ["jb"], jb, r, act.Identity, bias=-float(MAGIC * C // 16))
-    av(["f3"], ["sp0"], sp0, r, act.Identity, scale=4.0, bias=385.0)
-    av(["f3"], ["par16"], par16, par, act.Identity, scale=16.0)
-    av(["row", "jb"], ["jc"], T.jc[:], T.row[:], act.Identity, scale=16.0, bias=jb)
-    av(["row", "sp0"], ["spare"], T.spare[:], T.row[:, 0:4], act.Identity, bias=sp0)
+    av(["f3"], ["rh"], rh, r4, act.Identity, bias=0.5)
+    av(["f3"], ["nbc"], nb, r4, act.Identity, scale=2048.0)
+    av(["f3"], ["nbm"], nm, r4, act.Identity, scale=-2048.0)
+    av(["f3", "lift"], ["jb"], jb, r, act.Identity, scale=1.0 / C, bias=lift)
+    av(["gam0"], ["gam"], T.gam[:], T.gam0[:], act.Identity, bias=0.5)
+    av(["row", "rh"], ["keyc"], T.keyc[:], T.row[:, 0:4], act.Identity, bias=rh)
+    av(["row", "jb"], ["jc"], T.jc[:], T.row[:], act.Identity, scale=16.0 / C, bias=jb)
+    for a in range(WIDE, C, WIDE):
+        av(["c1"], ["c1_%d" % a], T.c1[:, a:a + WIDE], T.c1[:, 0:WIDE], act.Copy)
+    av(["keyc"], ["spare"], T.spare[:], T.keyc[:], act.Identity, bias=384.5)
+
+    HB = {1: 6, 3: 7}
+    FREE = 6
+    PB, KB = [1, 2, 3][:NR], [4, 0, 1][:NR]
+
+    def state_run(t, i):
+        every = [(j, k) for j in range(NR) for k in range(2)]
+        for j, k in every[2 * i + AHEAD if i else 0:2 * (i + 1) + AHEAD]:
+            lo, hi = RUNS[j]
+            n, b = hi - lo, (1, 3)[k]
+            tt(["ps%d" % HB[b], "gb%d" % j], ["st%d_%d_%d" % (t, j, b)], T["st%d" % t][:, 4 * lo + b:4 * hi:4], ps(HB[b], lo, hi),
+               T.gb[:, 2 * lo + n * k:2 * lo + n * k + n], op.add)
+
+    def state_gather(i):
+        lo, hi = RUNS[i]
+        av(["dgb", "kl2"], ["gb%d" % i], T.gb[:, 2 * lo:2 * hi], T.dg[:, 2 * M:4 * M].indirect(T.kl2[:, lo // 8:hi // 8]), act.Copy)
+
+    def state_own(t):
+        for k, b in enumerate((0, 2)):
+            tt(["dga", "keyl", "dh%d" % b], ["st%d_%d_%d" % (t, i, b) for i in range(NR)], T["st%d" % t][:, b:4 * C:4],
+               T.dg[:, M * k:M * k + M].indirect(T.keyl[:]), T.dh[:, C * b:C * b + C], op.add)
+
+    def quant_run(t, i):
+        lo, hi = RUNS[i]
+        rd = ["st%d_%d_%d" % (t, i, b) for b in range(4)] if t else ["st0_%d" % i]
+        quant(rd, ["qx%d_%d" % (t, i)], T["qx%d" % t][:, lo:hi], T["sx%d" % t][:, lo:hi], T["st%d" % t][:, 4 * lo:4 * hi])
 
     for t in range(ROUNDS):
-        st, nxt = T["st%d" % t], T["st%d" % (t + 1)]
         qx, sx = T["qx%d" % t], T["sx%d" % t]
         qa, sa, qc, sc = T["qa%d" % t], T["sa%d" % t], T["qc%d" % t], T["sc%d" % t]
         qz, sz, qh, sh = T["qz%d" % t], T["sz%d" % t], T["qh%d" % t], T["sh%d" % t]
-        win, flag = T["win%d" % t], T["flag%d" % t]
-        kx, kw, kf = "qx%d" % t, "win%d" % t, "flag%d" % t
-        new = ["st%d_%d" % (t, b) for b in range(4)]
-        kxa, kxb = kx + "a", kx + "b"
+        wf = T["wf%d" % t]
+        kw = "wf%d" % t
+        kx = ["qx%d_%d" % (t, i) for i in range(NR)]
+        L = NR - 1
 
-        quant(new if t else ["st0a"], [kxa], qx[:, 0:h], sx[:, 0:h], st[:, 0:4 * h])
-        mm(["qu", kxa], 4, h, T.qu[:], T.su[:], qx[:, 0:h], sx[:, 0:h])
-        quant(new if t else ["st0b"], [kxb], qx[:, h:C], sx[:, h:C], st[:, 4 * h:4 * C])
-        mm(["qu", kxb], 5, h, T.qu[:], T.su[:], qx[:, h:C], sx[:, h:C])
+        def hot(i, qs):
+            lo, hi = RUNS[i]
+            for q in qs:
+                ts(["kb%d" % i, "keyc"], ["oh%d_%d" % (q, i)], T.oh[:, C * q + lo:C * q + hi], T.kb[:, lo:hi],
+                   T.keyc[:, q:q + 1], 0.5, op.is_equal, op.mult)
 
-        def own(b):
-            mm([kxa, kxb, "qe%d" % b], b, C, T.qe[:, 128 * b:128 * b + 128], T.se[:, 128 * b:128 * b + 128], qx[:], sx[:])
+        def own(b, bk):
+            if t == 0:
+                quant(["zh"], ["qj%d" % b], T.qj[:, 128 * b:128 * b + 128], T.sj[:, 128 * b:128 * b + 128], T.zh[:, 3 - b:515 - b])
+            halved(kx, bk, b, C, qx[:], sx[:])
+            av(["ps%d" % bk], ["dh%d" % b], T.dh[:, C * b:C * b + C], ps(bk, 0, C), act.Copy)
 
-        def half(b):
-            av(["ps%d" % b], ["dh%d" % b], T.dh[:, C * b:C * b + C], ps(b, 0, C), act.Copy, scale=0.5)
-        own(0)
-        half(0)
-        ts(["ps4", "bitz0"], ["bitsa"], T.bits[:, 0:4 * h:4], ps(4, 0, h), 0.0, None, op.is_gt)
-        ts(["ps5", "bitz1"], ["bitsb"], T.bits[:, 4 * h:4 * C:4], ps(5, 0, h), 0.0, None, op.is_gt)
-        for i, nm in enumerate("ab"):
-            lo, hi = h * i, h * i + h
-            quant(["bits" + nm], ["qb" + nm], T.qb[:, lo:hi], T.sb[:, lo:hi], T.bits[:, 4 * lo:4 * hi])
-            mm(["qk", "qb" + nm], 4 + i, h, T.qk[:, 0:128], T.sk[:, 0:128], T.qb[:, lo:hi], T.sb[:, lo:hi])
-            mm(["qk", "qb" + nm], 6 + i, h, T.qk[:, 0:128], T.sk[:, 0:128], T.qb[:, lo:hi], T.sb[:, lo:hi])
-            av(["ps%d" % (6 + i)], ["kb" + nm], T.kb[:, lo:hi], ps(6 + i, 0, h), act.Identity, bias=64.0)
-        mm(["qk", "qba", "qbb"], 1, C, T.qk[:, 128:256], T.sk[:, 128:256], T.qb[:], T.sb[:])
-        own(2)
-        own(3)
-        av(["ps1", "sgb"], ["junk", "bsum"], T.junk[:], ps(1, 0, C), act.Sign, scale=-1.0, bias=sgb, accum_out=T.bsum[:, 0:1])
-        av(["bsum"], ["cs0"], T.cs[:, 15:16], T.bsum[:, 0:1], act.Copy, scale=0.5)
-        av(["ps1", "nb"], ["pen"], T.pen[:], ps(1, 0, C), act.Abs, scale=1024.0, bias=nb)
-        own(1)
+        if t:
+            for i in range(NR):
+                state_gather(i)
+            state_own(t)
+        for i, (lo, hi) in enumerate(RUNS):
+            if t:
+                state_run(t, i)
+            quant_run(t, i)
+            mm(["qu", kx[i]], PB[i], hi - lo, T.qu[:], T.su[:], qx[:, lo:hi], sx[:, lo:hi])
+            av(["ps%d" % PB[i]], ["bits%d" % i], T.bits[:, 4 * lo:4 * hi:4], ps(PB[i], 0, hi - lo), act.Sign, bias=-TINY)
+        for i, (lo, hi) in enumerate(RUNS):
+            quant(["bits%d" % i], ["qb%d" % i], T.qb[:, lo:hi], T.sb[:, lo:hi], T.bits[:, 4 * lo:4 * hi])
+            mm(["qk", "qb%d" % i], KB[i], hi - lo, T.qk[:], T.sk[:], T.qb[:, lo:hi], T.sb[:, lo:hi])
+            av(["ps%d" % KB[i]], ["kb%d" % i], T.kb[:, lo:hi], ps(KB[i], 0, hi - lo), act.Identity, bias=32.0)
+        kbk = ["kb%d" % i for i in range(NR)]
+        av(kbk + ["nbc"], ["junk", "bs"], T.junk[:], T.kb[:], act.Sign, scale=-2048.0, bias=nb, accum_out=T.bsum[:, 0:1])
+        av(["bs"], ["cs0"], T.cs[:, 15:16], T.bsum[:, 0:1], act.Identity, scale=0.5)
+        av(kbk + ["nbm"], ["pen"], T.pen[:], T.kb[:], act.Relu, scale=2048.0, bias=nm)
+        kd = T.ks[:, 15:C:16]
+        for i in range(L):
+            hot(i, range(4))
+        scan(["c1"] + ["c1_%d" % a for a in range(WIDE, C, WIDE)] + kbk, ["ks"], T.ks[:], T.c1[:], T.kb[:], 0.0, op.add, op.max)
+        hot(L, range(3))
+        ts(["ks", "lift"], ["qi"], T.qi[:], kd, lift, FOUR - 2.0, op.add, op.add)
+        tt(["ks", "jc"], ["qf"], T.qf[:], kd, T.jc[:], op.add)
+        hot(L, [3])
         if t == 0:
-            av(["ni", "par16"], ["num"], T.num[:], T.ni[:], act.Identity, bias=par16)
-        half(2)
-        half(3)
-        half(1)
-        if t == 0:
-            av(["c2"], ["flag0"], T.flag0[:, 0:C], T.c2[:], act.Relu)
-            av(["c2"], ["atz"], T.at[:, 0:256], T.c2[:, 0:256], act.Relu)
-        kbk = ["kba", "kbb"]
-        av(kbk, ["klf"], T.klf[:], T.kb[:], act.Identity, bias=-64.0)
-        dma("s", ["klf"], [], T.kl[8 * t:8 * t + 8, :], T.klf[0:128:16, :])
+            fill(["neg"], T.num[:, C:C + M], BIG)
+            fill(["mxz"], T.mx[:, C:4 * MS:MS], 0.0)
+            av(["ni", "f3"], ["num"], T.num[:, 0:C], T.ni[:], act.Identity, bias=par16)
+            av(["wf0z"], ["atz"], T.at[:, 0:256], T.wf0[:, 0:256], act.Copy)
+            av(["wf0z"], ["flag0"], T.wf0[:, FL:FL + C], T.wf0[:, 0:C], act.Copy)
+        tt(["qf", "qi"], ["qg"], T.qg[:], T.qf[:], T.qi[:], op.subtract)
 
-        def hot(q):
-            ts(kbk + ["keyc"], ["oh%d" % q], T.oh[:, C * q:C * q + C], T.kb[:], T.keyc[:, q:q + 1], 0.5, op.is_equal, op.mult)
-        ts(["ps4", "f3"], ["oh0a"], T.oh[:, 0:h], ps(4, 0, h), r, 0.5, op.is_equal, op.mult)
-        if t == 0:
-            ts(["jm", "f3"], ["c1"], T.c1[:], T.jm[:], r, 2.0, op.not_equal, op.mult)
-        ts(["ps5", "f3"], ["oh0b"], T.oh[:, h:C], ps(5, 0, h), r, 0.5, op.is_equal, op.mult)
-        scan(["c1"] + kbk, ["ks"], T.ks[:], T.c1[:], T.kb[:], 0.0, op.mult, op.max)
-        hot(1)
-        ts(["ks", "pwi"], ["qi"], T.qi[:], T.ks[:, 15:C:16], pwi, MAGIC - 64 - 7.5, op.mult, op.add)
-        hot(2)
-        ts(["qi"], ["qf"], T.qf[:], T.qi[:], float(C // 16), None, op.mult)
-        hot(3)
-        tt(["qf", "jc"], ["qg"], T.qg[:], T.qf[:], T.jc[:], op.add)
-        scan(["oh0a", "oh0b", "oh1", "oh2", "oh3", "cs0"], ["cs"], T.cs[:, 16:16 + 4 * C], T.oh[:], T.oh[:], T.cs[:, 15:16], op.add, op.add)
-        cp(["qg"], ["ql"], T.ql[:], T.qg[:])
+        scan(["oh%d_%d" % (q, i) for q in range(4) for i in range(NR)] + ["cs0"], ["cs"], T.cs[:, 16:16 + 4 * C], T.oh[:], T.oh[:],
+             T.cs[:, 15:16], op.add, op.add)
         ends, starts = T.cs[:, 15 + C:16 + 4 * C:C], T.cs[:, 15:16 + 3 * C:C]
-        tt(["cs", "ql", "pen"], ["vv"], T.vv[:], T.cs[:, 16:16 + 4 * C].indirect(T.ql[:]), T.pen[:], op.subtract)
+        ts(["qg"], ["ql"], T.ql[:], T.qg[:], float(C), C * (FOUR - 0.5) + 0.25, op.mult, op.add)
+        run("v", ["pen"], ["pent"], lambda: g.vector.transpose(T.pent[:], T.pen[:]))
+        cp(["cs", "ql"], ["vv"], T.vv[:], T.cs[:, 16:16 + 4 * C].indirect(T.ql[:]))
         tt(["cs", "cs0"], ["em"], T.em[:], ends, starts, op.is_equal)
+        own(1, HB[1])
         run("v", ["vv"], ["vtr"], lambda: g.vector.transpose(T.vtr[:], T.vv[:]))
         tt(["em", "spare"], ["emd"], T.emd[:], T.em[:], T.spare[:], op.mult)
-        scan(["c2", "vtr"], ["ms"], T.ms[:], T.c2[:], T.vtr[:], 0.0, op.add, op.max)
+        own(0, 3)
+        scan(["pent", "vtr"], ["ms"], T.ms[:], T.pent[:], T.vtr[:], 0.0, op.add, op.min)
         tt(["emd", "cs", "cs0"], ["stf"], T.stf[:], T.emd[:], starts, op.add)
-        ts(["ms"], ["pb"], T.pb[:], T.ms[:, 15:C:16], MAGIC + 191 - 7.5, None, op.add)
-        tt(["ms", "gam"], ["pc"], T.pc[:], T.ms[:, 15:C:16], T.gam[:], op.add)
-        tt(["pb", "pc"], ["pd"], T.pd[:], T.pb[:], T.pc[:], op.add)
+        own(2, 5)
+        tt(["ms", "gam"], ["pb"], T.pb[:], T.ms[:, 15:C:16], T.gam[:], op.add)
+        ts(["stf"], ["fl"], T.pl[:, 24:28], T.stf[:], 192.0 + FL, None, op.add)
+        own(3, HB[3])
+        tt(["pb", "ms"], ["pd"], T.pd[:], T.pb[:], T.ms[:, 15:C:16], op.add)
         tt(["emd", "cs"], ["enf"], T.enf[:], T.emd[:], ends, op.add)
-        cp(["pd"], ["pl"], T.pl[:], T.pd[:])
-        ts(["stf"], ["fl"], T.fl[:], T.stf[:], 192.0, None, op.add)
-        cp(["pl", "num"], [kw], win[:].indirect(T.pl[:]), T.num[:])
-        run("v", [kw], ["wtr"], lambda: g.vector.transpose(T.wtr[:], win[:]))
-        tt(["wtr"], ["srcf"], T.srcf[:], T.wtr[:, 0:2 * C:32], T.wtr[:, 16:2 * C:32], op.add)
+        ts(["pd"], ["pl"], T.pl[:, 0:24], T.pd[:], 191.0 - MAGIC, None, op.add)
         ts(["enf"], ["el"], T.el[:], T.enf[:], 191.0, float(C), op.add, op.min)
+        av(kbk, ["klf"], T.klf[:], T.kb[:], act.Identity, bias=-0.5)
+        dma("s", ["klf"], [], T.kl[8 * t:8 * t + 8, :], T.klf[0:128:16, :])
+        cp(["pl", "fl", "num", "neg", "wf%dz" % t, "flag%d" % t], [kw], wf[:].indirect(T.pl[:]), T.num[:])
+        run("v", [kw], ["wtr"], lambda: g.vector.transpose(T.wtr[:], wf[:, 0:FL]))
+        tt(["wtr"], ["srcf"], T.srcf[:], T.wtr[:, 0:2 * C:32], T.wtr[:, 16:2 * C:32], op.add)
         ts(["srcf"], ["sl"], T.sl[:], T.srcf[:], 192.0, None, op.add)
 
-        for b in range(1, 4):
-            av(["dh%d" % b, "sl"], ["ds%d" % b], T.ds[:, C * b:C * b + C], T.dh[:, C * b:C * b + C].indirect(T.sl[:]), act.Copy)
-        cp(["fl", "neg"], [kf], flag[:].indirect(T.fl[:]), T.neg[:])
-        cp(["dh0", "sl"], ["ds0"], T.ds[:, 0:C], T.dh[:, 0:C].indirect(T.sl[:]))
-        for b in (1, 0, 2, 3):
-            scan([kf, "ds%d" % b], ["mx%d" % b], T.mx[:, MS * b:MS * b + C], flag[:, 0:C], T.ds[:, C * b:C * b + C], 0.0, op.add, op.max)
-            if b == 2:
-                ts(["mx0", "mxz", "el"], ["at0"], T.at[:, 256:512:4], T.mx[:, 0:C + 1].indirect(T.el[:]), 2.0, None, op.mult)
-        for b in (1, 2, 3):
-            src = T.mx[:, MS * b:MS * b + C + 1].indirect(T.el[:])
-            out = T.at[:, 256 + b:512:4]
-            if b < 3:
+        def pick(q, b, lo, hi, ko):
+            out, src = T.ds[:, C * b + lo:C * b + hi], T.dh[:, C * b:C * b + C].indirect(T.sl[:, lo // 16:hi // 16])
+            if q == "a":
+                av(["dh%d" % b, "sl"], [ko], out, src, act.Copy)
+            else:
+                cp(["dh%d" % b, "sl"], [ko], out, src)
+
+        def most(b, rd):
+            scan([kw] + rd, ["mx%d" % b], T.mx[:, MS * b:MS * b + C], wf[:, FL:FL + C], T.ds[:, C * b:C * b + C], 0.0, op.add, op.max)
+
+        def cell(q, b):
+            src, out = T.mx[:, MS * b:MS * b + C + 1].indirect(T.el[:]), T.at[:, 256 + b:512:4]
+            if q == "a":
                 av(["mx%d" % b, "mxz", "el"], ["at%d" % b], out, src, act.Copy, scale=2.0)
             else:
                 ts(["mx%d" % b, "mxz", "el"], ["at%d" % b], out, src, 2.0, None, op.mult)
+        pick("a", 1, 0, C, "ds1")
+        pick("v", 0, 0, C, "ds0")
+        pick("a", 2, 0, C, "ds2")
+        pick("v", 3, SPLIT, C, "ds3b")
+        pick("a", 3, 0, SPLIT, "ds3a")
+        for b in range(4):
+            most(b, ["ds%d" % b] if b < 3 else ["ds3b", "ds3a"])
+        for b, q in enumerate(CELL):
+            cell(q, b)
         ka = "qa%d" % t
         quant(["at0", "at1", "at2", "at3", "atz"], [ka], qa[:, 0:128], sa[:, 0:128], T.at[:])
 
-        order("g", [ka], [])
-        for buf, cast, one in ((qa, True, "onec%d" % t), (sa, False, "ones%d" % t)):
-            def vw(a, z):
-                return buf[:, a:z].bitcast(dt.uint8) if cast else buf[:, a:z]
-            g.remote_dma_fused([
-                RemoteDMATransfer(dst_ids=[dst(mate), dst(across)], dma_engine_mask=off_mask, remote_sem=T.sem[one],
-                                  src=vw(M, 2 * M), dsts=[vw(3 * M, 4 * M), vw(4 * M, 5 * M)]),
-                RemoteDMATransfer(dst_ids=[dst(sib)], dma_engine_mask=on_mask, remote_sem=T.sem[one],
-                                  src=vw(M, 2 * M), dst=vw(2 * M, 3 * M)),
-            ], local_sem=T.sem.sent)
-            writer["land1c" if cast else "land1s"] = (one, 2 * n_off + n_on)
-            top[one] = 2 * n_off + n_on
-        top["sent"] = top.get("sent", 0) + 2 * (n_off + n_on)
+        def vx(bb, z, a, e):
+            return bb[:, a:e].bitcast(dt.uint8) if z == "c" else bb[:, a:e]
 
-        ts(["ks", "pwi"], ["keyl"], T.keyl[:], T.ks[:, 15:C:16], pwi, 64.0, op.mult, op.subtract)
+        def send(rd, trs):
+            order("g", rd, [])
+            g.remote_dma_fused([RemoteDMATransfer(dst_ids=[dst(c) for c in cs], dma_engine_mask=m, remote_sem=T.sem[s], src=src, dsts=ds)
+                                for cs, m, s, src, ds in trs], local_sem=T.sem.sent)
+            for cs, m, s, src, ds in trs:
+                n = bin(m).count("1")
+                top["sent"] = top.get("sent", 0) + n
+                top[s] = top.get(s, 0) + n * len(cs)
+                writer[s] = (s, top[s])
+        sfx = str(t)
+        both = ((qa, qc, "c"), (sa, sc, "s"))
+        for buf, lnd, z in both:
+            send([ka], [([mate, across], off_mask, "off" + z + sfx, vx(buf, z, M, 2 * M), [vx(buf, z, 3 * M, 4 * M), vx(buf, z, 4 * M, 5 * M)]),
+                        ([sib], on_mask, "sib" + z + sfx, vx(buf, z, M, 2 * M), [vx(buf, z, 2 * M, 3 * M)])])
+
+        def onward(buf, lnd, z):
+            return ([sib], on_mask, "fwd" + sfx, vx(buf, z, 3 * M, 5 * M), [vx(lnd, z, 0, 2 * M)])
+
+        def outward(buf, lnd, z):
+            return ([fourth], off_mask, "fth" + sfx, vx(buf, z, M, 3 * M), [vx(lnd, z, 2 * M, 4 * M)])
+        if APART:
+            for a in both:
+                send(["sib" + a[2] + sfx], [outward(*a)])
+            for a in both:
+                send(["off" + a[2] + sfx], [onward(*a)])
+        else:
+            for a in both:
+                send(["sib" + a[2] + sfx, "off" + a[2] + sfx], [outward(*a), onward(*a)])
+
+        if t == 0:
+            ts(["zh"], ["zt"], T.zt[:], T.zh[:], 2.0, None, op.mult)
+            for b in range(4):
+                quant(["zt"], ["qe%d" % b], T.qe[:, 128 * b:128 * b + 128], T.se[:, 128 * b:128 * b + 128], T.zt[:, 3 - b:515 - b])
+        ts(["ks", "lift"], ["na"], T.na[:], kd, lift, 16.0, op.add, op.mult)
+        ts(["qi"], ["nb"], T.nb[:], T.qi[:], -15.75, 15.75 * FOUR - 8.0, op.mult, op.add)
+        tt(["na", "nb"], ["nc"], T.nc[:], T.na[:], T.nb[:], op.add)
+        cp(["nc"], ["keyl"], T.keyl[:], T.nc[:])
+        for i, (lo, hi) in enumerate(RUNS):
+            n = (hi - lo) // 16
+            for k in range(2):
+                ts(["nc"], ["kl2_%d_%d" % (i, k)], T.kl2[:, lo // 8 + n * k:lo // 8 + n * k + n], T.nc[:, lo // 16:hi // 16], 64.0 * k, None, op.add)
+        writer["kl2"] = writer["kl2_%d_1" % (NR - 1)]
         if t == 0:
             fill(["ztz"], T.ztile[:, 256:512], 0.0)
-            fill(["gtz"], T.gtile[:, 256:512], 0.0)
-            fill(["win1"], T.win1[:], 0.0)
-            fill(["flag1"], T.flag1[:, 0:C], 0.0)
+            fill(["wf1z", "flag1"], T.wf1[:, 0:FL + C], 0.0)
             quant(["vt"], ["qv"], T.qv[:], T.sv[:], T.vt[:])
-            ts(["zt"], ["zh"], T.zh[:], T.zt[:], 0.5, None, op.mult)
-            for b in (2, 3):
-                quant(["zh"], ["qj%d" % b], T.qj[:, 128 * b - 256:128 * b - 128], T.sj[:, 128 * b - 256:128 * b - 128], T.zh[:, 3 - b:515 - b])
-
-        twoa, twob = "twoa%d" % t, "twob%d" % t
-        for buf, lnd, cast in ((qa, qc, True), (sa, sc, False)):
-            order("g", ["land1c" if cast else "land1s"], [])
-
-            def vx(bb, a, z):
-                return bb[:, a:z].bitcast(dt.uint8) if cast else bb[:, a:z]
-            g.remote_dma_fused([
-                RemoteDMATransfer(dst_ids=[dst(fourth)], dma_engine_mask=off_mask, remote_sem=T.sem[twob],
-                                  src=vx(buf, M, 3 * M), dst=vx(lnd, 2 * M, 4 * M)),
-                RemoteDMATransfer(dst_ids=[dst(sib)], dma_engine_mask=on_mask, remote_sem=T.sem[twoa],
-                                  src=vx(buf, 3 * M, 5 * M), dst=vx(lnd, 0, 2 * M)),
-            ], local_sem=T.sem.sent)
-        top["sent"] += 2 * (n_off + n_on)
-        writer["land2a"], writer["land2b"] = (twoa, 2 * n_on), (twob, 2 * n_off)
-        top[twoa], top[twob] = 2 * n_on, 2 * n_off
 
         def slot(i, b):
             return T.acc[:, (4 * i + b) * M:(4 * i + b + 1) * M]
 
-        def more(i, b0, c0):
+        def batch(i, rd, rq, rs):
+            bk = [(2 * i + b) % FREE for b in range(4)]
             for b in range(4):
-                out, ko = (slot(i, b), "acc%d_%d" % (i, b)) if i < 7 else (T.ztile[:, b:256:4], "zt_%d" % b)
-                tt(["ps%d" % (b0 + b), "acc%d_%d" % (i - 1, b)], [ko], out, ps(b0 + b, c0, c0 + M), slot(i - 1, b), op.max)
-        unpack([ka, "land1c", "land1s"], 0, 4 * M, qa[:, M:5 * M], sa[:, M:5 * M])
+                whole(rd, bk[b], b, 2 * M, rq, rs)
+            for j in range(max(i, 1), i + 2):
+                for b in range(4):
+                    out, ko = (slot(j, b), "acc%d_%d" % (j, b)) if j < 7 else (T.ztile[:, b:256:4], "zt_%d" % b)
+                    tt(["ps%d" % bk[b], "acc%d_%d" % (j - 1, b)], [ko], out, ps(bk[b], M * (j - i), M * (j - i) + M), slot(j - 1, b), op.max)
         for b in range(4):
-            cp(["ps%d" % b], ["acc0_%d" % b], slot(0, b), ps(b, 0, M))
-        for i in range(1, 4):
-            more(i, 0, M * i)
-        unpack(["land2a"], 4, 2 * M, qc[:, 0:2 * M], sc[:, 0:2 * M])
-        more(4, 4, 0)
-        more(5, 4, M)
-        unpack(["land2b"], 0, 2 * M, qc[:, 2 * M:4 * M], sc[:, 2 * M:4 * M])
-        more(6, 0, 0)
-        more(7, 0, M)
+            whole([ka], b, b, 2 * M, qa[:, 0:2 * M], sa[:, 0:2 * M])
+            av(["ps%d" % b], ["acc0_%d" % b], slot(0, b), ps(b, M, 2 * M), act.Copy)
+        batch(0, [ka, "sibc" + sfx, "sibs" + sfx], qa[:, M:3 * M], sa[:, M:3 * M])
+        batch(2, ["offc" + sfx, "offs" + sfx], qa[:, 3 * M:5 * M], sa[:, 3 * M:5 * M])
+        if APART:
+            batch(4, ["fth" + sfx], qc[:, 2 * M:4 * M], sc[:, 2 * M:4 * M])
+            batch(6, ["fwd" + sfx], qc[:, 0:2 * M], sc[:, 0:2 * M])
+        else:
+            batch(4, ["fwd" + sfx], qc[:, 0:2 * M], sc[:, 0:2 * M])
+            batch(6, ["fth" + sfx], qc[:, 2 * M:4 * M], sc[:, 2 * M:4 * M])
 
         kz, kh = "qz%d" % t, "qh%d" % t
         quant(["zt_0", "zt_1", "zt_2", "zt_3", "ztz"], [kz], qz[:], sz[:], T.ztile[:])
         for b in range(4):
             mm([kz, "qw", "sw"], b, 128, T.qw[:, 128 * b:128 * b + 128], T.sw[:, 128 * b:128 * b + 128], qz[:], sz[:])
         for b in range(4):
-            out = T.gtile[:, b:256:4]
-            if b % 2 == 0:
-                av(["ps%d" % b], ["gt%d" % b], out, ps(b, 0, M), act.Relu, scale=0.015625)
-            else:
-                ts(["ps%d" % b], ["gt%d" % b], out, ps(b, 0, M), 0.0, 0.015625, op.max, op.mult)
-        quant(["gt0", "gt1", "gt2", "gt3", "gtz"], [kh], qh[:], sh[:], T.gtile[:])
-        unpack([kh], 4, 128, qh[:], sh[:])
-        for b in (2, 3):
-            mm([kxa, kxb, "qj%d" % b], b, C, T.qj[:, 128 * b - 256:128 * b - 128], T.sj[:, 128 * b - 256:128 * b - 128], qx[:], sx[:])
-        ts(["ps4"], ["dg0"], T.dg[:, 0:M], ps(4, 0, M), 0.5, None, op.mult)
-        for b in (1, 2, 3):
-            av(["ps%d" % (4 + b)], ["dg%d" % b], T.dg[:, M * b:M * b + M], ps(4 + b, 0, M), act.Copy, scale=0.5)
-        for b in (2, 3):
-            av(["dg%d" % b, "keyl"], ["gb%d" % b], T.gb[:, C * (b - 2):C * (b - 1)], T.dg[:, M * b:M * b + M].indirect(T.keyl[:]), act.Copy)
-        for b in range(4):
-            ko, out = "st%d_%d" % (t + 1, b), nxt[:, b:4 * C:4]
-            if b < 2:
-                tt(["dg%d" % b, "keyl", "dh%d" % b], [ko], out, T.dg[:, M * b:M * b + M].indirect(T.keyl[:]), T.dh[:, C * b:C * b + C], op.add)
-            else:
-                tt(["ps%d" % b, "gb%d" % b], [ko], out, ps(b, 0, C), T.gb[:, C * (b - 2):C * (b - 1)], op.add)
+            for k, out in enumerate((T.gtile[:, b:256:4], T.gtile[:, 256 + (b + 2) % 4:512:4])):
+                if RELU[b] == "a":
+                    av(["ps%d" % b], ["gt%d_%d" % (b, k)], out, ps(b, 0, M), act.Relu, scale=0.015625)
+                else:
+                    ts(["ps%d" % b], ["gt%d_%d" % (b, k)], out, ps(b, 0, M), 0.0, 0.015625, op.max, op.mult)
+        quant(["gt%d_%d" % (b, k) for b in range(4) for k in range(2)], [kh], qh[:], sh[:], T.gtile[:])
+        halved([kh], 4, 0, 128, qh[:], sh[:])
+        halved([kh], 0, 1, 128, qh[:], sh[:])
+        av(["ps4"], ["dga"], T.dg[:, 0:2 * M], ps(4, 0, 2 * M), act.Copy)
+        av(["ps0"], ["dgb"], T.dg[:, 2 * M:4 * M], ps(0, 0, 2 * M), act.Copy)
 
-    qx, sx, st = T["qx%d" % ROUNDS], T["sx%d" % ROUNDS], T["st%d" % ROUNDS]
-    new = ["st%d_%d" % (ROUNDS, b) for b in range(4)]
-    quant(new, ["qfa"], qx[:, 0:h], sx[:, 0:h], st[:, 0:4 * h])
-    mm(["qfa", "qv"], 0, h, T.qv[:], T.sv[:], qx[:, 0:h], sx[:, 0:h])
-    quant(new, ["qfb"], qx[:, h:C], sx[:, h:C], st[:, 4 * h:4 * C])
-    mm(["qfb", "qv"], 1, h, T.qv[:], T.sv[:], qx[:, h:C], sx[:, h:C])
-    av(["ps0"], ["yb0"], T.yb[:, 0:h], ps(0, 0, h), act.Copy)
-    cp(["ps1"], ["yb1"], T.yb[:, h:C], ps(1, 0, h))
-    dma("s", ["qfa", "qfb"], [], T.oc[:], qx[:].bitcast(dt.uint8))
-    dma("a", ["yb0", "yb1"], [], T.y[:], T.yb[:])
-    for k in range(4):
-        dma("s" if k < 3 else "a", ["qfa", "qfb"], [], T.osc[4 * k:4 * k + 4, :], sx[32 * k:32 * k + 4, :])
+    t = ROUNDS
+    qx, sx = T["qx%d" % t], T["sx%d" % t]
+    every = ["qx%d_%d" % (t, i) for i in range(NR)]
+    for i in range(NR):
+        state_gather(i)
+    state_own(t)
+    for i, (lo, hi) in enumerate(RUNS):
+        state_run(t, i)
+        quant_run(t, i)
+        mm([every[i], "qv"], 1 + i, hi - lo, T.qv[:], T.sv[:], qx[:, lo:hi], sx[:, lo:hi])
+        if i < NR - 1:
+            av(["ps%d" % (1 + i)], ["yb%d" % i], T.yb[:, lo:hi], ps(1 + i, 0, hi - lo), act.Copy)
+        else:
+            cp(["ps%d" % (1 + i)], ["yb%d" % i], T.yb[:, lo:hi], ps(1 + i, 0, hi - lo))
+    dma("s", every, [], T.oc[:], qx[:].bitcast(dt.uint8))
+    dma("a", ["yb%d" % i for i in range(NR)], [], T.y[:], T.yb[:])
+    for k, q in enumerate(SQ):
+        dma(q, every, [], T.osc[4 * k:4 * k + 4, :], sx[32 * k:32 * k + 4, :])
 
     for s in sorted(top):
         if max([n for (q, z), n in waited.items() if z == s] + [0]) < top[s]:

@@ -7,17 +7,43 @@ ROUNDS = 2
 MS = 400
 BIG = -1.0e20
 MAGIC = 3072
-FOUR = 768
+LIFT = 2048.0
 TINY = 2.0 ** -120
 RUNS = [(0, 128), (128, 256), (256, 384)]
+MARK = [(0,), (1,), (2,)]
 FL = 2 * C
-SPLIT = 96
-APART = False
-CELL = "aaaa"
+PLACE = 160
+PICK = [("a", 3, 0, 192), ("v", 0, 0, 192), ("a", 2, 0, C), ("v", 3, 192, C), ("a", 1, 0, C), ("v", 0, 192, C)]
+CELL = "aaav"
 RELU = "vava"
-SQ = "ssag"
-AHEAD = 2
-WIDE = max(hi - lo for lo, hi in RUNS)
+BACK = "vava"
+FUSE = [(0, 2), (0, 2), (0, 2)]
+SIDE = {0: 0, 2: 1, 1: 2, 3: 3}
+SQ = "gssa"
+ORDER = """
+pidx.1 ut.1 st0_0.1 wf0z.1 jm.1 i31.1 i30.1 i32.1 wtz.1 row.1 st0_1.1 bits0.1 gam0.1 f3.1 ji.1 lt6.1 zhz.1 rh.1 st0_2.1 bits2.1 dbl.1 zi.1 c0.1 qu.1
+wk.1 qx0_0.1 ni.1 bits1.1 low.1 wt0.1 zh.1 ps1.1 qx0_1.1 wt1.1 jb2.1 ps2.1 bits0.2 qw.1 qx0_2.1 c2.1 qk.1 vt.1 bits1.2 qb0.1 ps3.1 qq.1 nbm.1 sw.1
+ps4.1 qb1.1 bits2.2 qj3.1 ps0.1 keyc.1 ps1.2 kb0.1 qb2.1 cs0.1 ps2.2 kq0.1 nbc.1 oh1_0.1 kb1.1 ps3.2 oh0_0.1 oh3_0.1 gam.1 ps4.2 oh2_0.1 kq1.1 ps7.1
+kb2.1 oh1_1.1 oh3_1.1 pen0.1 oh2_1.1 oh0_1.1 kq2.1 jc.1 oh3_2.1 bs.1 oh2_2.1 oh0_2.1 oh1_2.1 qf.1 cs.1 pen1.1 spare.1 bh.1 num.1 ql.1 pent0.1 pent1.1
+vv1.1 em.1 vv0.1 neg.1 mxz.1 atz.1 vtr1.1 vtr0.1 flag0.1 ms1.1 ms0.1 qj2.1 pb0.1 zt.1 emd.1 ps5.1 pd0.1 qj0.1 pl0.1 qj1.1 dh3.1 ps0.2 wf0.1 dh2.1
+ps6.1 stf.1 enf.1 bh2.1 dh0.1 wtr0.1 wtr1.1 dh1.1 srcf0.1 fl.1 el.1 srcf1.1 sl0.1 ff0.1 sl1.1 ds0.1 ds1.1 ds3.1 ds4.1 ds5.1 ds2.1 mx3.1 mx1.1 mx0.1
+at1.1 mx2.1 at0.1 at3.1 qe0.1 at2.1 c1_0.1 c1_256.1 qa0.1 qe1.1 c1_128.1 offc0.1 lift.1 nb.1 klf.1 ks.1 gtz.1 qe2.1 qe3.1 klf.2 na.1 nc.1 offs0.1
+kl3_1_0.1 kl3_1_1.1 kl3_0_1.1 wf1z.1 kl3_2_0.1 ps7.2 ps5.2 fth0.1 ps6.2 fth0.2 ps4.3 acc0_1.1 acc0_3.1 ps1.3 kl3_2_1.1 acc1_1.1 ps0.3 acc0_0.1
+acc1_3.1 acc0_2.1 ps3.3 kl3_0_0.1 wf1z.2 acc1_0.1 ps2.3 acc1_2.1 acc2_1.1 ps5.3 acc2_0.1 ztz.1 acc2_3.1 ps4.4 acc2_2.1 acc3_1.1 acc3_0.1 flag1.1 ps6.3
+acc3_2.1 acc3_3.1 ps7.3 wf1z.3 acc4_0.1 acc4_1.1 ps1.4 acc4_2.1 ps0.4 acc4_3.1 acc5_0.1 acc5_1.1 ps2.4 acc5_2.1 acc5_3.1 ps3.4 acc6_0.1 acc6_1.1
+acc6_2.1 ps7.4 acc6_3.1 zt_0.1 zt_1.1 zt_2.1 zt_3.1 keyl.1 qz0.1 ps2.5 ps3.5 ps0.5 gt2_0.1 ps1.5 gt3_0.1 gt0_0.1 gt1_0.1 qh0.1 qv.1 ps4.5 ps1.6 ps0.6
+dg0.1 ps2.6 dg2.1 st1_0_0.1 ps6.4 dg1.1 dg3.1 st1_0_2.1 gb0.1 gb2.1 st1_0_3.1 st1_0_1.1 gb1.1 st1_2_1.1 st1_2_3.1 qx1_0.1 st1_1_1.1 st1_1_3.1 ps1.7
+qx1_2.1 qx1_1.1 bits0.3 ps3.6 ps2.7 qb0.2 bits2.3 bits1.3 ps4.6 qb2.2 ps0.7 qb1.2 kb0.2 ps3.7 kq0.2 ps2.8 oh1_0.2 ps1.8 kb2.2 oh0_0.2 oh2_0.2 flag1.2
+ps4.7 oh3_0.2 kq1.2 ps0.8 oh1_2.2 kb1.2 oh2_2.2 kq2.2 pen1.2 oh3_2.2 pen0.2 oh0_2.2 oh2_1.2 ps5.4 oh1_1.2 qf.2 bs.2 oh0_1.2 oh3_1.2 ql.2 ps6.5 cs.2
+bh.2 ps7.5 pent0.2 vv0.2 vv1.2 em.2 pent1.2 bh2.2 vtr0.2 dh2.2 vtr1.2 ms0.2 ms1.2 dh1.2 pb0.2 emd.2 nb.2 dh0.2 pd0.2 stf.2 pl0.2 fl.2 enf.2 dh3.2
+wf1.1 wtr1.2 wtr0.2 srcf1.2 srcf0.2 el.2 sl1.2 sl0.2 ff1.1 ds3.2 ds2.2 ds5.2 ds0.2 ds1.2 mx2.2 ds4.2 mx3.2 mx0.2 at2.2 mx1.2 at0.2 at3.2 at1.2 klf.3
+qa1.1 ks.2 offc1.1 klf.4 offs1.1 na.2 nc.2 ps5.5 kl3_2_1.2 kl3_1_1.2 ps6.6 kl3_0_0.2 kl3_1_0.2 kl3_0_1.2 fth1.1 ps7.6 acc0_1.2 fth1.2 ps4.8 acc0_2.2
+ps2.9 acc1_2.2 ps1.9 acc0_0.2 acc1_1.2 acc0_3.2 ps3.8 kl3_2_0.2 acc1_0.2 ps0.9 acc1_3.2 acc2_2.2 ps6.7 acc2_1.2 acc2_3.2 ps5.6 acc2_0.2 keyl.2
+acc3_1.2 ps7.7 acc3_2.2 acc3_3.2 ps4.9 acc3_0.2 acc4_1.2 ps2.10 acc4_2.2 acc4_3.2 ps1.10 acc4_0.2 acc5_1.2 acc5_2.2 ps3.9 acc5_3.2 acc5_0.2 ps0.10
+acc6_1.2 acc6_2.2 ps7.8 acc6_3.2 acc6_0.2 zt_1.2 zt_2.2 zt_3.2 zt_0.2 ps6.8 qz1.1 ps2.11 ps3.10 ps0.11 gt2_0.2 ps1.11 gt3_0.2 gt0_0.2 gt1_0.2 qh1.1
+ps1.12 ps4.10 ps0.12 dg2.2 ps2.12 dg0.2 st2_0_2.1 dg1.2 dg3.2 st2_0_0.1 gb0.2 gb1.2 st2_0_1.1 st2_0_3.1 gb2.2 st2_1_3.1 st2_1_1.1 qx2_0.1 st2_2_3.1
+st2_2_1.1 ps1.13 qx2_1.1 qx2_2.1 yb0.1 ps2.13 qx2_0.2 qx2_0.3 ps3.11 yb1.1 yb2.1 qx2_0.4 yb2.2 qx2_0.5 qx2_0.6
+"""
 CODE, U8, BF, F32, I32, U16 = "float8_e4m3fn_x4", "uint8", "bfloat16", "float32", "int32", "uint16"
 
 SCRATCH = {"ps%d" % _b: ("psum", [128, 512], F32) for _b in range(8)}
@@ -25,19 +51,19 @@ for _n, _w, _d in [
         ("st0", 4 * C, BF), ("st1", 4 * C, BF), ("st2", 4 * C, BF), ("ut", 512, BF), ("vt", 512, BF),
         ("qu", 128, CODE), ("su", 128, U8), ("qv", 128, CODE), ("sv", 128, U8), ("qw", 512, CODE), ("sw", 512, U8),
         ("pidx", 4, I32), ("i3", 4, I32), ("f3", 4, F32), ("row", 24, F32), ("dbl", 16, F32), ("cst", 16, F32),
-        ("keyc", 4, BF), ("spare", 4, F32), ("jc", 24, F32), ("gam0", 24, F32), ("gam", 24, F32), ("rb", 2, BF),
-        ("zi", 128, BF), ("zt", 520, BF), ("zh", 520, BF), ("ji", 128, BF), ("wt", 512, BF),
-        ("qe", 512, CODE), ("se", 512, U8), ("qj", 512, CODE), ("sj", 512, U8), ("qk", 128, CODE), ("sk", 128, U8),
-        ("jm", WIDE + 16, BF), ("c0", 2 * WIDE, BF), ("c1", C, BF), ("ni", C, BF), ("num", C + M, BF),
+        ("keyc", 4, BF), ("spare", 4, F32), ("jc", 24, F32), ("gam0", 24, F32), ("gam", 24, F32),
+        ("zi", 128, BF), ("zt", 520, BF), ("zh", 520, BF), ("ji", 128, BF), ("wt", 520, BF),
+        ("qe", 512, CODE), ("se", 512, U8), ("qj", 512, CODE), ("sj", 512, U8), ("qk", 256, CODE), ("sk", 256, U8),
+        ("jm", 128, BF), ("c0", 128, BF), ("c1", C, BF), ("c2", 128, BF), ("ni", C, BF), ("num", C + M, BF),
         ("bits", 4 * C, BF), ("qb", C, CODE), ("sb", C, U8), ("dh", 4 * C, BF), ("kb", C, BF), ("junk", C, BF),
-        ("bsum", 8, F32), ("pen", C, BF), ("pent", C, BF), ("klf", C, F32), ("oh", 4 * C, BF), ("cs", 16 + 4 * C, BF), ("ks", C, BF),
-        ("qi", 24, BF), ("qf", 24, F32), ("qg", 24, F32), ("ql", 24, U16), ("na", 24, F32), ("nb", 24, F32), ("nc", 24, F32),
-        ("keyl", 24, U16), ("kl2", 48, U16),
-        ("vv", C, BF), ("vtr", C, BF), ("ms", C, BF), ("pb", 24, BF), ("pd", 24, F32), ("pl", 28, U16),
-        ("wf0", FL + 848, BF), ("wf1", FL + 848, BF), ("wtr", 2 * C, BF), ("srcf", 24, F32), ("sl", 24, U16),
+        ("bsum", 8, F32), ("pen", C, BF), ("pent", C, BF), ("klf", C, F32), ("oh", 4 * C, BF), ("cs", 16 + 4 * C, BF),
+        ("ks", C, F32), ("kq", C, BF),
+        ("qf", 24, F32), ("ql", 24, U16), ("na", 24, F32), ("nb", 24, F32), ("nc", 96, F32), ("keyl", 96, U16),
+        ("vv", C, BF), ("vtr", C, BF), ("ms", C, BF), ("pb", 24, BF), ("pd", 24, F32), ("pl", 24, U16), ("fl", 4, U16),
+        ("wf0", FL, BF), ("wf1", FL, BF), ("ff0", 848, BF), ("ff1", 848, BF), ("wtr", 2 * C, BF), ("srcf", 24, F32), ("sl", 24, U16),
         ("em", 4, F32), ("emd", 4, F32), ("stf", 4, F32), ("enf", 4, F32), ("el", 4, U16),
         ("ds", 4 * C, BF), ("mx", 4 * MS, BF), ("at", 512, BF),
-        ("acc", 8 * 4 * M, BF), ("ztile", 512, BF), ("gtile", 512, BF), ("dg", 4 * M, BF), ("gb", 2 * C, BF),
+        ("acc", 8 * 4 * M, BF), ("ztile", 512, BF), ("gtile", 512, BF), ("dg", 4 * M, BF), ("gb", 3 * C, BF),
         ("yb", C, F32)]:
     SCRATCH[_n] = ("sbuf", [128, _w], _d)
 for _t in range(ROUNDS + 1):
@@ -53,64 +79,31 @@ SEMAPHORES = (["ev", "ea", "ep", "eg", "sent"]
               + ["d%d" % i for i in range(24)])
 
 
+def arrange(steps):
+    if not ORDER:
+        return steps
+    at = {n: i for i, n in enumerate(ORDER.split())}
+    return sorted(steps, key=lambda s: at[s[0]])
+
+
 def rank_program(g, core, T, topo):
     rank = T.rank_of(core)
     if rank is None:
         return
     op, act = AluOpType, ActivationFunctionType
     Q = {"v": g.vector, "a": g.scalar, "p": g.tensor, "g": g, "s": g.sync}
-    count = {"v": 0, "a": 0, "p": 0, "g": 0}
-    waited, top, writer, readers, bank, ndma = {}, {}, {}, {}, {}, [0]
+    steps, seen = [], {}
 
-    def wait(q, tok):
-        s, n = tok
-        if waited.get((q, s), 0) < n:
-            Q[q].wait_ge(T.sem[s], n)
-            waited[(q, s)] = n
-
-    def order(q, rd, wr):
-        need = {}
-
-        def add(tok):
-            if tok is not None:
-                need[tok[0]] = max(need.get(tok[0], 0), tok[1])
-        for k in rd:
-            add(writer[k])
-        for k in wr:
-            add(writer.get(k))
-            for tok in readers.get(k, []):
-                add(tok)
-        for k in list(rd) + list(wr):
-            if k.startswith("ps"):
-                for e, tok in bank.get(k, {}).items():
-                    if e != q:
-                        add(tok)
-        for s in sorted(need):
-            wait(q, (s, need[s]))
-
-    def note(q, rd, wr, tok):
-        top[tok[0]] = max(top.get(tok[0], 0), tok[1])
-        for k in rd:
-            readers.setdefault(k, []).append(tok)
-        for k in wr:
-            writer[k] = tok
-            readers[k] = []
-        for k in list(rd) + list(wr):
-            if k.startswith("ps"):
-                bank.setdefault(k, {})[q] = tok
+    def step(kind, q, rd, wr, call):
+        k = (list(wr) + list(rd))[0]
+        seen[k] = seen.get(k, 0) + 1
+        steps.append(("%s.%d" % (k, seen[k]), kind, q, list(rd), list(wr), call))
 
     def run(q, rd, wr, call):
-        order(q, rd, wr)
-        count[q] += 1
-        call().then_inc(T.sem["e" + q], 1)
-        note(q, rd, wr, ("e" + q, count[q]))
+        step("run", q, rd, wr, call)
 
     def dma(q, rd, wr, out, in_):
-        order(q, rd, wr)
-        s = "d%d" % ndma[0]
-        ndma[0] += 1
-        Q[q].dma_start(out, in_).then_inc(T.sem[s], 16)
-        note(q, rd, wr, (s, 16))
+        step("dma", q, rd, wr, lambda: Q[q].dma_start(out, in_))
 
     def ts(rd, wr, out, in0, s1, s2, o0, o1=None):
         if o1 is None:
@@ -130,11 +123,20 @@ def rank_program(g, core, T, topo):
     def scan(rd, wr, out, d0, d1, init, o0, o1):
         run("v", rd, wr, lambda: g.vector.tensor_tensor_scan(out, d0, d1, init, o0, o1))
 
+    def turn(rd, wr, out, in_):
+        run("v", rd, wr, lambda: g.vector.transpose(out, in_))
+
     def quant(rd, wr, qo, so, in_):
         run("v", rd, wr, lambda: g.vector.quantize_mx(qo, so, in_))
 
     def av(rd, wr, out, in_, func, **kw):
         run("a", rd, wr, lambda: g.scalar.activation(out, in_, func, **kw))
+
+    def move(q, rd, wr, out, in_):
+        if q == "a":
+            av(rd, wr, out, in_, act.Copy)
+        else:
+            cp(rd, wr, out, in_)
 
     def mm(rd, b, n, lq, ls, rq, rs):
         run("p", rd, ["ps%d" % b], lambda: g.tensor.matmul_mx(T["ps%d" % b][:, 0:n], lq, ls, rq, rs, True, True))
@@ -167,78 +169,98 @@ def rank_program(g, core, T, topo):
         rid, pid = topo.addr(c, core)
         return DstId(rid=rid, pnc=pid)
 
+    def send(rd, trs):
+        def call():
+            g.remote_dma_fused([RemoteDMATransfer(dst_ids=[dst(c) for c in cs], dma_engine_mask=m, remote_sem=T.sem[s], src=src, dsts=ds)
+                                for cs, m, s, src, ds in trs], local_sem=T.sem.sent)
+            return [(s, bin(m).count("1"), len(cs)) for cs, m, s, src, ds in trs]
+        step("send", "g", rd, [tr[2] for tr in trs], call)
+
     NR = len(RUNS)
+    L = NR - 1
     dma("a", [], ["ut"], T.ut[:], T.u[:])
     for i, (lo, hi) in enumerate(RUNS):
         dma("s", [], ["st0_%d" % i], T.st0[:, 4 * lo:4 * hi], T.x[:, 4 * lo:4 * hi])
-    dma("s", ["st0_%d" % (NR - 1)], ["qw"], T.qw[:].bitcast(dt.uint8), T.wc[:])
-    dma("s", [], ["sw"], T.sw[:], T.ws[:])
+    dma("s", ["st0_%d" % L], ["qw"], T.qw[:].bitcast(dt.uint8), T.wc[:])
+    dma("s", ["st0_%d" % L], ["sw"], T.sw[:], T.ws[:])
+    dma("g", ["st0_%d" % L], ["vt"], T.vt[:], T.v[:])
 
     iota(["pidx"], T.pidx[:, 0:1], [[0, 1]], 0, 4, False)
     iota(["row"], T.row[:], [[1, 24]], 0, 0)
     iota(["ji"], T.ji[:], [[1, 8], [0, 16]], 0, 0)
+    iota(["jm"], T.jm[:], [[0, 8], [1, 16]], 0, 0)
     iota(["zi"], T.zi[:], [[1, 128]], 0, -1)
-    iota(["jm"], T.jm[:], [[0, WIDE // 16 + 1], [1, 16]], 0, 0)
     iota(["gam0"], T.gam0[:], [[0, 12], [16, 2]], MAGIC + 183, 0)
     iota(["ni"], T.ni[:], [[32, 12], [0, 2], [1, 16]], -192, 0)
 
-    fill(["wf0z"], T.wf0[:, 0:FL], 0.0)
-    dma("g" if "g" in SQ else "s", [], ["vt"], T.vt[:], T.v[:])
+    fill(["wf0z"], T.wf0[:], 0.0)
     for i, (lo, hi) in enumerate(RUNS):
         av(["wf0z"], ["bits%d" % i], T.bits[:, 4 * lo:4 * hi], T.wf0[:, 0:4 * (hi - lo)], act.Copy)
     ts(["pidx"], ["i30"], T.i3[:, 0:1], T.pidx[:, 0:1], 2, 15, op.arith_shift_right, op.bitwise_and)
     ts(["pidx"], ["i31"], T.i3[:, 1:2], T.pidx[:, 0:1], 6, None, op.arith_shift_right)
     ts(["pidx"], ["i32"], T.i3[:, 2:3], T.pidx[:, 0:1], 2, 16, op.arith_shift_right, op.bitwise_and)
-    ts(["pidx"], ["i33"], T.i3[:, 3:4], T.pidx[:, 0:1], 63, None, op.bitwise_and)
     fill(["wtz"], T.wt[:], 0.0)
-    cp(["i30", "i31", "i32", "i33"], ["f3"], T.f3[:], T.i3[:])
-    r, grp, par16, r4 = T.f3[:, 0:1], T.f3[:, 1:2], T.f3[:, 2:3], T.f3[:, 3:4]
-    rb = T.rb[:, 0:1]
-    cp(["i30"], ["rb"], rb, T.i3[:, 0:1])
+    cp(["i30", "i31", "i32"], ["f3"], T.f3[:, 0:3], T.i3[:, 0:3])
+    r, grp, par16 = T.f3[:, 0:1], T.f3[:, 1:2], T.f3[:, 2:3]
     fill(["zhz"], T.zh[:], 0.0)
-    wk, lift, nb, jb, rh, nm = [T.cst[:, i:i + 1] for i in range(6)]
+    wk, lift, nb, rh, nm, low, wq = [T.cst[:, i:i + 1] for i in range(7)]
     ts(["row", "f3"], ["dbl"], T.dbl[:, 0:15], T.row[:, 0:15], r, 1.0, op.is_lt, op.add)
     ts(["f3"], ["lt6"], T.dbl[:, 15:16], r, 6.0, 0.5, op.is_lt, op.mult)
-    ts(["f3"], ["lift"], lift, r, 15.0, -64.0, op.is_lt, op.mult)
+    ts(["f3"], ["low"], low, r, 2.0, 1.0, op.is_lt, op.mult)
     ts(["zi", "zhz"], ["zh"], T.zh[:, 3:515:4], T.zi[:], 0.0, 0.5, op.is_equal, op.mult)
     run("v", ["dbl", "lt6"], ["wk"], lambda: g.vector.tensor_reduce(wk, T.dbl[:], AxisListType.X, op.mult))
-    ts(["jm", "rb"], ["c0a"], T.c0[:, 0:WIDE], T.jm[:, 16:16 + WIDE], rb, -4096.0, op.is_equal, op.mult)
-    ts(["jm", "rb"], ["c0b"], T.c0[:, WIDE:2 * WIDE], T.jm[:, 15:15 + WIDE], rb, 64.0, op.is_equal, op.mult)
+    ts(["jm", "f3"], ["c0"], T.c0[:], T.jm[:], r, -32.0 * LIFT, op.is_equal, op.mult)
     ts(["ji", "f3", "wk", "wtz"], ["wt0"], T.wt[:, 0:512:4], T.ji[:], grp, wk, op.is_equal, op.mult)
-    tt(["c0a", "c0b"], ["c1"], T.c1[:, 0:WIDE], T.c0[:, 0:WIDE], T.c0[:, WIDE:2 * WIDE], op.add)
-    quant(["wt0"], ["qk"], T.qk[:], T.sk[:], T.wt[:])
+    ts(["wt0", "low"], ["wt1"], T.wt[:, 1:512:4], T.wt[:, 0:512:4], low, None, op.mult)
+    quant(["wt0", "wt1"], ["qk"], T.qk[:, 0:128], T.sk[:, 0:128], T.wt[:, 0:512])
+    quant(["wt0", "wt1"], ["qq"], T.qk[:, 128:256], T.sk[:, 128:256], T.wt[:, 1:513])
     quant(["ut"], ["qu"], T.qu[:], T.su[:], T.ut[:])
-    av(["f3"], ["rh"], rh, r4, act.Identity, bias=0.5)
-    av(["f3"], ["nbc"], nb, r4, act.Identity, scale=2048.0)
-    av(["f3"], ["nbm"], nm, r4, act.Identity, scale=-2048.0)
-    av(["f3", "lift"], ["jb"], jb, r, act.Identity, scale=1.0 / C, bias=lift)
+    av(["f3"], ["rh"], rh, r, act.Identity, scale=4.0, bias=0.5)
+    av(["f3"], ["nbc"], nb, r, act.Identity, scale=8192.0)
+    av(["f3"], ["nbm"], nm, r, act.Identity, scale=-8192.0)
+    av(["f3"], ["lift"], lift, r, act.Identity, scale=LIFT / 4 + 63.0, bias=23.5 - 15.0 * (LIFT / 4 + 63.0))
+    av(["f3"], ["jb2"], wq, r, act.Identity, scale=4.0 + 1.0 / C, bias=1.5 - 60.0)
+    av(["c0"], ["c2"], T.c2[:], T.c0[:], act.Identity, scale=4.0 / LIFT, bias=4.0)
     av(["gam0"], ["gam"], T.gam[:], T.gam0[:], act.Identity, bias=0.5)
     av(["row", "rh"], ["keyc"], T.keyc[:], T.row[:, 0:4], act.Identity, bias=rh)
-    av(["row", "jb"], ["jc"], T.jc[:], T.row[:], act.Identity, scale=16.0 / C, bias=jb)
-    for a in range(WIDE, C, WIDE):
-        av(["c1"], ["c1_%d" % a], T.c1[:, a:a + WIDE], T.c1[:, 0:WIDE], act.Copy)
+    av(["row", "jb2"], ["jc"], T.jc[:], T.row[:], act.Identity, scale=16.0 / C, bias=wq)
+    for a in range(0, C, 128):
+        av(["c0"], ["c1_%d" % a], T.c1[:, a:a + 128], T.c0[:], act.Identity, bias=LIFT)
     av(["keyc"], ["spare"], T.spare[:], T.keyc[:], act.Identity, bias=384.5)
+    for b in range(4):
+        quant(["zh"], ["qj%d" % b], T.qj[:, 128 * b:128 * b + 128], T.sj[:, 128 * b:128 * b + 128], T.zh[:, 3 - b:515 - b])
+    av(["wf0z"], ["neg"], T.num[:, C:C + M], T.wf0[:, 0:M], act.Identity, bias=BIG)
+    av(["wf0z"], ["mxz"], T.mx[:, C:4 * MS:MS], T.wf0[:, 0:4], act.Copy)
+    av(["wf0z"], ["cs0"], T.cs[:, 15:16], T.wf0[:, 0:1], act.Identity, bias=-192.0)
+    av(["ni", "f3"], ["num"], T.num[:, 0:C], T.ni[:], act.Identity, bias=par16)
+    av(["wf0z"], ["atz"], T.at[:, 0:256], T.wf0[:, 0:256], act.Copy)
+    av(["wf0z"], ["flag0"], T.ff0[:, 0:C], T.wf0[:, 0:C], act.Copy)
 
-    HB = {1: 6, 3: 7}
-    FREE = 6
-    PB, KB = [1, 2, 3][:NR], [4, 0, 1][:NR]
+    HB = {2: 5, 1: 6, 3: 7}
+    FREE = 8
+    PB, KB, QB = [1, 2, 3], [4, 1, 3], [0, 2, 4]
+    apart = [[b for b in (2, 1, 3) if b not in FUSE[i]] for i in range(NR)]
+    first = [0 if 2 in apart[i] else 2 for i in range(NR)]
+    at = [24 + sum(len(apart[j]) * (RUNS[j][1] - RUNS[j][0]) // 16 for j in range(i)) for i in range(NR + 1)]
 
-    def state_run(t, i):
-        every = [(j, k) for j in range(NR) for k in range(2)]
-        for j, k in every[2 * i + AHEAD if i else 0:2 * (i + 1) + AHEAD]:
-            lo, hi = RUNS[j]
-            n, b = hi - lo, (1, 3)[k]
-            tt(["ps%d" % HB[b], "gb%d" % j], ["st%d_%d_%d" % (t, j, b)], T["st%d" % t][:, 4 * lo + b:4 * hi:4], ps(HB[b], lo, hi),
-               T.gb[:, 2 * lo + n * k:2 * lo + n * k + n], op.add)
-
-    def state_gather(i):
-        lo, hi = RUNS[i]
-        av(["dgb", "kl2"], ["gb%d" % i], T.gb[:, 2 * lo:2 * hi], T.dg[:, 2 * M:4 * M].indirect(T.kl2[:, lo // 8:hi // 8]), act.Copy)
-
-    def state_own(t):
-        for k, b in enumerate((0, 2)):
-            tt(["dga", "keyl", "dh%d" % b], ["st%d_%d_%d" % (t, i, b) for i in range(NR)], T["st%d" % t][:, b:4 * C:4],
-               T.dg[:, M * k:M * k + M].indirect(T.keyl[:]), T.dh[:, C * b:C * b + C], op.add)
+    def state(t):
+        st = T["st%d" % t]
+        for i, (lo, hi) in enumerate(RUNS):
+            n = len(apart[i]) * (hi - lo)
+            av(["dg0", "dg2"] * (first[i] == 0) + ["dg1", "dg3", "keyl"], ["gb%d" % i],
+               T.gb[:, 3 * lo:3 * lo + n], T.dg[:, M * first[i]:4 * M].indirect(T.keyl[:, at[i]:at[i + 1]]), act.Copy)
+        for b in range(4):
+            rs = [i for i in range(NR) if b in FUSE[i]]
+            if rs:
+                lo, hi = RUNS[rs[0]][0], RUNS[rs[-1]][1]
+                tt(["dg%d" % b, "keyl", "dh%d" % b], ["st%d_%d_%d" % (t, i, b) for i in rs], st[:, 4 * lo + b:4 * hi:4],
+                   T.dg[:, M * SIDE[b]:M * SIDE[b] + M].indirect(T.keyl[:, lo // 16:hi // 16]), T.dh[:, C * b + lo:C * b + hi], op.add)
+        for i, (lo, hi) in enumerate(RUNS):
+            for k, b in enumerate(apart[i]):
+                a = 3 * lo + k * (hi - lo)
+                tt(["ps%d" % HB[b], "gb%d" % i], ["st%d_%d_%d" % (t, i, b)], st[:, 4 * lo + b:4 * hi:4], ps(HB[b], lo, hi),
+                   T.gb[:, a:a + hi - lo], op.add)
+            quant_run(t, i)
 
     def quant_run(t, i):
         lo, hi = RUNS[i]
@@ -249,221 +271,214 @@ def rank_program(g, core, T, topo):
         qx, sx = T["qx%d" % t], T["sx%d" % t]
         qa, sa, qc, sc = T["qa%d" % t], T["sa%d" % t], T["qc%d" % t], T["sc%d" % t]
         qz, sz, qh, sh = T["qz%d" % t], T["sz%d" % t], T["qh%d" % t], T["sh%d" % t]
-        wf = T["wf%d" % t]
-        kw = "wf%d" % t
+        wf, ff = T["wf%d" % t], T["ff%d" % t]
+        kw, kf = "wf%d" % t, "ff%d" % t
         kx = ["qx%d_%d" % (t, i) for i in range(NR)]
-        L = NR - 1
-
-        def hot(i, qs):
-            lo, hi = RUNS[i]
-            for q in qs:
-                ts(["kb%d" % i, "keyc"], ["oh%d_%d" % (q, i)], T.oh[:, C * q + lo:C * q + hi], T.kb[:, lo:hi],
-                   T.keyc[:, q:q + 1], 0.5, op.is_equal, op.mult)
-
-        def own(b, bk):
-            if t == 0:
-                quant(["zh"], ["qj%d" % b], T.qj[:, 128 * b:128 * b + 128], T.sj[:, 128 * b:128 * b + 128], T.zh[:, 3 - b:515 - b])
-            halved(kx, bk, b, C, qx[:], sx[:])
-            av(["ps%d" % bk], ["dh%d" % b], T.dh[:, C * b:C * b + C], ps(bk, 0, C), act.Copy)
 
         if t:
+            state(t)
+        else:
             for i in range(NR):
-                state_gather(i)
-            state_own(t)
+                quant_run(t, i)
         for i, (lo, hi) in enumerate(RUNS):
-            if t:
-                state_run(t, i)
-            quant_run(t, i)
             mm(["qu", kx[i]], PB[i], hi - lo, T.qu[:], T.su[:], qx[:, lo:hi], sx[:, lo:hi])
             av(["ps%d" % PB[i]], ["bits%d" % i], T.bits[:, 4 * lo:4 * hi:4], ps(PB[i], 0, hi - lo), act.Sign, bias=-TINY)
         for i, (lo, hi) in enumerate(RUNS):
+            n = hi - lo
             quant(["bits%d" % i], ["qb%d" % i], T.qb[:, lo:hi], T.sb[:, lo:hi], T.bits[:, 4 * lo:4 * hi])
-            mm(["qk", "qb%d" % i], KB[i], hi - lo, T.qk[:], T.sk[:], T.qb[:, lo:hi], T.sb[:, lo:hi])
-            av(["ps%d" % KB[i]], ["kb%d" % i], T.kb[:, lo:hi], ps(KB[i], 0, hi - lo), act.Identity, bias=32.0)
-        kbk = ["kb%d" % i for i in range(NR)]
-        av(kbk + ["nbc"], ["junk", "bs"], T.junk[:], T.kb[:], act.Sign, scale=-2048.0, bias=nb, accum_out=T.bsum[:, 0:1])
-        av(["bs"], ["cs0"], T.cs[:, 15:16], T.bsum[:, 0:1], act.Identity, scale=0.5)
-        av(kbk + ["nbm"], ["pen"], T.pen[:], T.kb[:], act.Relu, scale=2048.0, bias=nm)
-        kd = T.ks[:, 15:C:16]
-        for i in range(L):
-            hot(i, range(4))
-        scan(["c1"] + ["c1_%d" % a for a in range(WIDE, C, WIDE)] + kbk, ["ks"], T.ks[:], T.c1[:], T.kb[:], 0.0, op.add, op.max)
-        hot(L, range(3))
-        ts(["ks", "lift"], ["qi"], T.qi[:], kd, lift, FOUR - 2.0, op.add, op.add)
-        tt(["ks", "jc"], ["qf"], T.qf[:], kd, T.jc[:], op.add)
-        hot(L, [3])
-        if t == 0:
-            fill(["neg"], T.num[:, C:C + M], BIG)
-            fill(["mxz"], T.mx[:, C:4 * MS:MS], 0.0)
-            av(["ni", "f3"], ["num"], T.num[:, 0:C], T.ni[:], act.Identity, bias=par16)
-            av(["wf0z"], ["atz"], T.at[:, 0:256], T.wf0[:, 0:256], act.Copy)
-            av(["wf0z"], ["flag0"], T.wf0[:, FL:FL + C], T.wf0[:, 0:C], act.Copy)
-        tt(["qf", "qi"], ["qg"], T.qg[:], T.qf[:], T.qi[:], op.subtract)
+            mm(["qk", "qb%d" % i], KB[i], n, T.qk[:, 0:128], T.sk[:, 0:128], T.qb[:, lo:hi], T.sb[:, lo:hi])
+            mm(["qq", "qb%d" % i], QB[i], n, T.qk[:, 128:256], T.sk[:, 128:256], T.qb[:, lo:hi], T.sb[:, lo:hi])
+            av(["ps%d" % KB[i]], ["kb%d" % i], T.kb[:, lo:hi], ps(KB[i], 0, n), act.Identity, bias=32.0)
+            scan(["c2", "ps%d" % QB[i]], ["kq%d" % i], T.kq[:, lo:hi], T.c2[:, 0:n], ps(QB[i], 0, n), 0.0, op.add, op.max)
+        for rs in MARK:
+            lo, hi = RUNS[rs[0]][0], RUNS[rs[-1]][1]
+            for q in range(4):
+                ts(["kb%d" % i for i in rs] + ["keyc"], ["oh%d_%d" % (q, i) for i in rs], T.oh[:, C * q + lo:C * q + hi], T.kb[:, lo:hi],
+                   T.keyc[:, q:q + 1], 0.5, op.is_equal, op.mult)
+        kbk, kqk = ["kb%d" % i for i in range(NR)], ["kq%d" % i for i in range(NR)]
+        tt(kqk + ["jc"], ["qf"], T.qf[:], T.kq[:, 15:C:16], T.jc[:], op.add)
+        ts(["qf"], ["ql"], T.ql[:], T.qf[:], float(C), None, op.mult)
+        bh, bh2 = T.bsum[:, 1:2], T.bsum[:, 2:3]
+        av(kbk + ["nbc"], ["bs", "junk"], T.junk[:], T.kb[:], act.Sign, scale=-2048.0, bias=nb, accum_out=T.bsum[:, 0:1])
+        av(["bs"], ["bh"], bh, T.bsum[:, 0:1], act.Identity, scale=0.5, bias=192.0)
+        av(["bs"], ["bh2"], bh2, T.bsum[:, 0:1], act.Identity, scale=0.5, bias=383.0)
+        cut = RUNS[L][0]
+        for k, (lo, hi) in enumerate(((0, cut), (cut, C))):
+            av((kbk[:L], kbk[L:])[k] + ["nbm"], ["pen%d" % k], T.pen[:, lo:hi], T.kb[:, lo:hi], act.Relu, scale=2048.0, bias=nm)
+            turn(["pen%d" % k], ["pent%d" % k], T.pent[:, lo:hi], T.pen[:, lo:hi])
+        for b, bk in ((1, HB[1]), (0, 0), (2, HB[2]), (3, HB[3])):
+            halved(kx, bk, b, C, qx[:], sx[:])
+            av(["ps%d" % bk], ["dh%d" % b], T.dh[:, C * b:C * b + C], ps(bk, 0, C), act.Copy)
 
-        scan(["oh%d_%d" % (q, i) for q in range(4) for i in range(NR)] + ["cs0"], ["cs"], T.cs[:, 16:16 + 4 * C], T.oh[:], T.oh[:],
-             T.cs[:, 15:16], op.add, op.add)
+        scan(["oh%d_%d" % (q, i) for q in range(4) for i in range(NR)], ["cs"], T.cs[:, 16:16 + 4 * C], T.oh[:], T.oh[:],
+             -192.0, op.add, op.add)
         ends, starts = T.cs[:, 15 + C:16 + 4 * C:C], T.cs[:, 15:16 + 3 * C:C]
-        ts(["qg"], ["ql"], T.ql[:], T.qg[:], float(C), C * (FOUR - 0.5) + 0.25, op.mult, op.add)
-        run("v", ["pen"], ["pent"], lambda: g.vector.transpose(T.pent[:], T.pen[:]))
-        cp(["cs", "ql"], ["vv"], T.vv[:], T.cs[:, 16:16 + 4 * C].indirect(T.ql[:]))
+        win = T.cs[:, 16:16 + 4 * C]
         tt(["cs", "cs0"], ["em"], T.em[:], ends, starts, op.is_equal)
-        own(1, HB[1])
-        run("v", ["vv"], ["vtr"], lambda: g.vector.transpose(T.vtr[:], T.vv[:]))
+        ts(["cs", "ql", "bh"], ["vv0"], T.vv[:, 0:PLACE], win.indirect(T.ql[:, 0:PLACE // 16]), bh, None, op.add)
+        av(["cs", "ql", "bh"], ["vv1"], T.vv[:, PLACE:C], win.indirect(T.ql[:, PLACE // 16:C // 16]), act.Identity, bias=bh)
+        parts = [(0, PLACE), (PLACE, C)]
         tt(["em", "spare"], ["emd"], T.emd[:], T.em[:], T.spare[:], op.mult)
-        own(0, 3)
-        scan(["pent", "vtr"], ["ms"], T.ms[:], T.pent[:], T.vtr[:], 0.0, op.add, op.min)
+        for k, (lo, hi) in enumerate(parts):
+            turn(["vv%d" % k], ["vtr%d" % k], T.vtr[:, lo:hi], T.vv[:, lo:hi])
         tt(["emd", "cs", "cs0"], ["stf"], T.stf[:], T.emd[:], starts, op.add)
-        own(2, 5)
-        tt(["ms", "gam"], ["pb"], T.pb[:], T.ms[:, 15:C:16], T.gam[:], op.add)
-        ts(["stf"], ["fl"], T.pl[:, 24:28], T.stf[:], 192.0 + FL, None, op.add)
-        own(3, HB[3])
-        tt(["pb", "ms"], ["pd"], T.pd[:], T.pb[:], T.ms[:, 15:C:16], op.add)
+        for k, (lo, hi) in enumerate(parts):
+            scan(["pent0"] * (lo < cut) + ["pent1"] * (hi > cut) + ["vtr%d" % k], ["ms%d" % k], T.ms[:, lo:hi], T.pent[:, lo:hi],
+                 T.vtr[:, lo:hi], 0.0, op.add, op.min)
+        km = ["ms0", "ms1"]
+        ts(["stf", "bh"], ["fl"], T.fl[:], T.stf[:], bh, 192.0, op.add, op.add)
+        tt(km + ["gam"], ["pb0"], T.pb[:], T.ms[:, 15:C:16], T.gam[:], op.add)
+        tt(["pb0"] + km, ["pd0"], T.pd[:], T.pb[:], T.ms[:, 15:C:16], op.add)
+        ts(["pd0"], ["pl0"], T.pl[:], T.pd[:], 191.0 - MAGIC, None, op.add)
+        cp(["pl0", "num"], [kw, "wf%dz" % t], wf[:].indirect(T.pl[:]), T.num[:, 0:C])
         tt(["emd", "cs"], ["enf"], T.enf[:], T.emd[:], ends, op.add)
-        ts(["pd"], ["pl"], T.pl[:, 0:24], T.pd[:], 191.0 - MAGIC, None, op.add)
-        ts(["enf"], ["el"], T.el[:], T.enf[:], 191.0, float(C), op.add, op.min)
+        ts(["enf", "bh2"], ["el"], T.el[:], T.enf[:], bh2, float(C), op.add, op.min)
         av(kbk, ["klf"], T.klf[:], T.kb[:], act.Identity, bias=-0.5)
         dma("s", ["klf"], [], T.kl[8 * t:8 * t + 8, :], T.klf[0:128:16, :])
-        cp(["pl", "fl", "num", "neg", "wf%dz" % t, "flag%d" % t], [kw], wf[:].indirect(T.pl[:]), T.num[:])
-        run("v", [kw], ["wtr"], lambda: g.vector.transpose(T.wtr[:], wf[:, 0:FL]))
-        tt(["wtr"], ["srcf"], T.srcf[:], T.wtr[:, 0:2 * C:32], T.wtr[:, 16:2 * C:32], op.add)
-        ts(["srcf"], ["sl"], T.sl[:], T.srcf[:], 192.0, None, op.add)
+        cp(["fl", "neg", "flag%d" % t], [kf], ff[:].indirect(T.fl[:]), T.num[:, C:C + M])
+        twos = [(0, C // 2), (C // 2, C)]
+        for k, (lo, hi) in enumerate(twos):
+            a, z = lo // 16, hi // 16
+            turn([kw], ["wtr%d" % k], T.wtr[:, 2 * lo:2 * hi], wf[:, 2 * lo:2 * hi])
+            tt(["wtr%d" % k], ["srcf%d" % k], T.srcf[:, a:z], T.wtr[:, 2 * lo:2 * hi:32], T.wtr[:, 2 * lo + 16:2 * hi:32], op.add)
+            ts(["srcf%d" % k], ["sl%d" % k], T.sl[:, a:z], T.srcf[:, a:z], 192.0, None, op.add)
 
-        def pick(q, b, lo, hi, ko):
-            out, src = T.ds[:, C * b + lo:C * b + hi], T.dh[:, C * b:C * b + C].indirect(T.sl[:, lo // 16:hi // 16])
-            if q == "a":
-                av(["dh%d" % b, "sl"], [ko], out, src, act.Copy)
-            else:
-                cp(["dh%d" % b, "sl"], [ko], out, src)
-
-        def most(b, rd):
-            scan([kw] + rd, ["mx%d" % b], T.mx[:, MS * b:MS * b + C], wf[:, FL:FL + C], T.ds[:, C * b:C * b + C], 0.0, op.add, op.max)
-
-        def cell(q, b):
+        for k, (q, b, lo, hi) in enumerate(PICK):
+            move(q, ["dh%d" % b] + ["sl%d" % j for j, (a, z) in enumerate(twos) if a < hi and lo < z], ["ds%d" % k],
+                 T.ds[:, C * b + lo:C * b + hi], T.dh[:, C * b:C * b + C].indirect(T.sl[:, lo // 16:hi // 16]))
+        for b in range(4):
+            scan([kf] + ["ds%d" % k for k in range(len(PICK)) if PICK[k][1] == b], ["mx%d" % b], T.mx[:, MS * b:MS * b + C],
+                 ff[:, 0:C], T.ds[:, C * b:C * b + C], 0.0, op.add, op.max)
+        for b, q in enumerate(CELL):
             src, out = T.mx[:, MS * b:MS * b + C + 1].indirect(T.el[:]), T.at[:, 256 + b:512:4]
             if q == "a":
                 av(["mx%d" % b, "mxz", "el"], ["at%d" % b], out, src, act.Copy, scale=2.0)
             else:
                 ts(["mx%d" % b, "mxz", "el"], ["at%d" % b], out, src, 2.0, None, op.mult)
-        pick("a", 1, 0, C, "ds1")
-        pick("v", 0, 0, C, "ds0")
-        pick("a", 2, 0, C, "ds2")
-        pick("v", 3, SPLIT, C, "ds3b")
-        pick("a", 3, 0, SPLIT, "ds3a")
-        for b in range(4):
-            most(b, ["ds%d" % b] if b < 3 else ["ds3b", "ds3a"])
-        for b, q in enumerate(CELL):
-            cell(q, b)
         ka = "qa%d" % t
         quant(["at0", "at1", "at2", "at3", "atz"], [ka], qa[:, 0:128], sa[:, 0:128], T.at[:])
 
         def vx(bb, z, a, e):
             return bb[:, a:e].bitcast(dt.uint8) if z == "c" else bb[:, a:e]
-
-        def send(rd, trs):
-            order("g", rd, [])
-            g.remote_dma_fused([RemoteDMATransfer(dst_ids=[dst(c) for c in cs], dma_engine_mask=m, remote_sem=T.sem[s], src=src, dsts=ds)
-                                for cs, m, s, src, ds in trs], local_sem=T.sem.sent)
-            for cs, m, s, src, ds in trs:
-                n = bin(m).count("1")
-                top["sent"] = top.get("sent", 0) + n
-                top[s] = top.get(s, 0) + n * len(cs)
-                writer[s] = (s, top[s])
         sfx = str(t)
         both = ((qa, qc, "c"), (sa, sc, "s"))
         for buf, lnd, z in both:
             send([ka], [([mate, across], off_mask, "off" + z + sfx, vx(buf, z, M, 2 * M), [vx(buf, z, 3 * M, 4 * M), vx(buf, z, 4 * M, 5 * M)]),
                         ([sib], on_mask, "sib" + z + sfx, vx(buf, z, M, 2 * M), [vx(buf, z, 2 * M, 3 * M)])])
-
-        def onward(buf, lnd, z):
-            return ([sib], on_mask, "fwd" + sfx, vx(buf, z, 3 * M, 5 * M), [vx(lnd, z, 0, 2 * M)])
-
-        def outward(buf, lnd, z):
-            return ([fourth], off_mask, "fth" + sfx, vx(buf, z, M, 3 * M), [vx(lnd, z, 2 * M, 4 * M)])
-        if APART:
-            for a in both:
-                send(["sib" + a[2] + sfx], [outward(*a)])
-            for a in both:
-                send(["off" + a[2] + sfx], [onward(*a)])
-        else:
-            for a in both:
-                send(["sib" + a[2] + sfx, "off" + a[2] + sfx], [outward(*a), onward(*a)])
+        for buf, lnd, z in both:
+            send(["sib" + z + sfx, "off" + z + sfx],
+                 [([fourth], off_mask, "fth" + sfx, vx(buf, z, M, 3 * M), [vx(lnd, z, 2 * M, 4 * M)]),
+                  ([sib], on_mask, "fwd" + sfx, vx(buf, z, 3 * M, 5 * M), [vx(lnd, z, 0, 2 * M)])])
 
         if t == 0:
-            ts(["zh"], ["zt"], T.zt[:], T.zh[:], 2.0, None, op.mult)
+            av(["zh"], ["zt"], T.zt[:], T.zh[:], act.Copy, scale=2.0)
             for b in range(4):
                 quant(["zt"], ["qe%d" % b], T.qe[:, 128 * b:128 * b + 128], T.se[:, 128 * b:128 * b + 128], T.zt[:, 3 - b:515 - b])
-        ts(["ks", "lift"], ["na"], T.na[:], kd, lift, 16.0, op.add, op.mult)
-        ts(["qi"], ["nb"], T.nb[:], T.qi[:], -15.75, 15.75 * FOUR - 8.0, op.mult, op.add)
-        tt(["na", "nb"], ["nc"], T.nc[:], T.na[:], T.nb[:], op.add)
-        cp(["nc"], ["keyl"], T.keyl[:], T.nc[:])
+        scan(["c1_%d" % a for a in range(0, C, 128)] + kbk, ["ks"], T.ks[:], T.c1[:], T.kb[:], 0.0, op.add, op.max)
+        av(["ks", "lift"], ["na"], T.na[:], T.ks[:, 15:C:16], act.Identity, scale=0.25, bias=lift)
+        av(kqk, ["nb"], T.nb[:], T.kq[:, 15:C:16], act.Identity, scale=15.75)
+        tt(["na", "nb"], ["nc"], T.nc[:, 0:24], T.na[:], T.nb[:], op.add)
         for i, (lo, hi) in enumerate(RUNS):
             n = (hi - lo) // 16
-            for k in range(2):
-                ts(["nc"], ["kl2_%d_%d" % (i, k)], T.kl2[:, lo // 8 + n * k:lo // 8 + n * k + n], T.nc[:, lo // 16:hi // 16], 64.0 * k, None, op.add)
-        writer["kl2"] = writer["kl2_%d_1" % (NR - 1)]
+            for k, b in enumerate(apart[i]):
+                a = at[i] + n * k
+                av(["nc"], ["kl3_%d_%d" % (i, k)], T.nc[:, a:a + n], T.nc[:, lo // 16:hi // 16], act.Identity,
+                   bias=float(M * (SIDE[b] - first[i])))
+        cp(["nc"] + ["kl3_%d_%d" % (i, k) for i in range(NR) for k in range(len(apart[i]))], ["keyl"], T.keyl[:, 0:at[NR]], T.nc[:, 0:at[NR]])
         if t == 0:
-            fill(["ztz"], T.ztile[:, 256:512], 0.0)
-            fill(["wf1z", "flag1"], T.wf1[:, 0:FL + C], 0.0)
+            av(["atz"], ["ztz"], T.ztile[:, 256:512], T.at[:, 0:256], act.Copy)
+            for a in range(0, FL, 256):
+                av(["atz"], ["wf1z"], T.wf1[:, a:a + 256], T.at[:, 0:256], act.Copy)
+            for a in range(0, C, 192):
+                av(["atz"], ["flag1"], T.ff1[:, a:a + 192], T.at[:, 0:192], act.Copy)
             quant(["vt"], ["qv"], T.qv[:], T.sv[:], T.vt[:])
 
         def slot(i, b):
             return T.acc[:, (4 * i + b) * M:(4 * i + b + 1) * M]
 
         def batch(i, rd, rq, rs):
-            bk = [(2 * i + b) % FREE for b in range(4)]
+            bk = [(2 * i + b + 4) % FREE for b in range(4)]
             for b in range(4):
                 whole(rd, bk[b], b, 2 * M, rq, rs)
-            for j in range(max(i, 1), i + 2):
-                for b in range(4):
+                if i == 0:
+                    av(["ps%d" % bk[b]], ["acc0_%d" % b], slot(0, b), ps(bk[b], 0, M), act.Copy)
+                for j in range(max(i, 1), i + 2):
                     out, ko = (slot(j, b), "acc%d_%d" % (j, b)) if j < 7 else (T.ztile[:, b:256:4], "zt_%d" % b)
                     tt(["ps%d" % bk[b], "acc%d_%d" % (j - 1, b)], [ko], out, ps(bk[b], M * (j - i), M * (j - i) + M), slot(j - 1, b), op.max)
-        for b in range(4):
-            whole([ka], b, b, 2 * M, qa[:, 0:2 * M], sa[:, 0:2 * M])
-            av(["ps%d" % b], ["acc0_%d" % b], slot(0, b), ps(b, M, 2 * M), act.Copy)
         batch(0, [ka, "sibc" + sfx, "sibs" + sfx], qa[:, M:3 * M], sa[:, M:3 * M])
         batch(2, ["offc" + sfx, "offs" + sfx], qa[:, 3 * M:5 * M], sa[:, 3 * M:5 * M])
-        if APART:
-            batch(4, ["fth" + sfx], qc[:, 2 * M:4 * M], sc[:, 2 * M:4 * M])
-            batch(6, ["fwd" + sfx], qc[:, 0:2 * M], sc[:, 0:2 * M])
-        else:
-            batch(4, ["fwd" + sfx], qc[:, 0:2 * M], sc[:, 0:2 * M])
-            batch(6, ["fth" + sfx], qc[:, 2 * M:4 * M], sc[:, 2 * M:4 * M])
+        batch(4, ["fwd" + sfx], qc[:, 0:2 * M], sc[:, 0:2 * M])
+        batch(6, ["fth" + sfx], qc[:, 2 * M:4 * M], sc[:, 2 * M:4 * M])
+        for b in sorted(set(sum(apart, []))):
+            halved(kx, HB[b], b, C, qx[:], sx[:])
 
         kz, kh = "qz%d" % t, "qh%d" % t
         quant(["zt_0", "zt_1", "zt_2", "zt_3", "ztz"], [kz], qz[:], sz[:], T.ztile[:])
         for b in range(4):
             mm([kz, "qw", "sw"], b, 128, T.qw[:, 128 * b:128 * b + 128], T.sw[:, 128 * b:128 * b + 128], qz[:], sz[:])
+        if t == 0:
+            av(["atz"], ["gtz"], T.gtile[:, 256:512], T.at[:, 0:256], act.Copy)
         for b in range(4):
-            for k, out in enumerate((T.gtile[:, b:256:4], T.gtile[:, 256 + (b + 2) % 4:512:4])):
-                if RELU[b] == "a":
-                    av(["ps%d" % b], ["gt%d_%d" % (b, k)], out, ps(b, 0, M), act.Relu, scale=0.015625)
-                else:
-                    ts(["ps%d" % b], ["gt%d_%d" % (b, k)], out, ps(b, 0, M), 0.0, 0.015625, op.max, op.mult)
-        quant(["gt%d_%d" % (b, k) for b in range(4) for k in range(2)], [kh], qh[:], sh[:], T.gtile[:])
-        halved([kh], 4, 0, 128, qh[:], sh[:])
-        halved([kh], 0, 1, 128, qh[:], sh[:])
-        av(["ps4"], ["dga"], T.dg[:, 0:2 * M], ps(4, 0, 2 * M), act.Copy)
-        av(["ps0"], ["dgb"], T.dg[:, 2 * M:4 * M], ps(0, 0, 2 * M), act.Copy)
+            if RELU[b] == "a":
+                av(["ps%d" % b], ["gt%d_0" % b], T.gtile[:, b:256:4], ps(b, 0, M), act.Relu, scale=0.015625)
+            else:
+                ts(["ps%d" % b], ["gt%d_0" % b], T.gtile[:, b:256:4], ps(b, 0, M), 0.0, 0.015625, op.max, op.mult)
+        quant(["gt%d_0" % b for b in range(4)] + ["gtz"], [kh], qh[:], sh[:], T.gtile[:])
+        for b, bk in enumerate((4, 0, 1, 2)):
+            halved([kh], bk, b, 128, qh[:], sh[:])
+            move(BACK[b], ["ps%d" % bk], ["dg%d" % b], T.dg[:, M * SIDE[b]:M * SIDE[b] + M], ps(bk, 0, M))
 
     t = ROUNDS
     qx, sx = T["qx%d" % t], T["sx%d" % t]
     every = ["qx%d_%d" % (t, i) for i in range(NR)]
-    for i in range(NR):
-        state_gather(i)
-    state_own(t)
+    state(t)
     for i, (lo, hi) in enumerate(RUNS):
-        state_run(t, i)
-        quant_run(t, i)
         mm([every[i], "qv"], 1 + i, hi - lo, T.qv[:], T.sv[:], qx[:, lo:hi], sx[:, lo:hi])
-        if i < NR - 1:
-            av(["ps%d" % (1 + i)], ["yb%d" % i], T.yb[:, lo:hi], ps(1 + i, 0, hi - lo), act.Copy)
-        else:
-            cp(["ps%d" % (1 + i)], ["yb%d" % i], T.yb[:, lo:hi], ps(1 + i, 0, hi - lo))
+        move("a" if i < L else "v", ["ps%d" % (1 + i)], ["yb%d" % i], T.yb[:, lo:hi], ps(1 + i, 0, hi - lo))
     dma("s", every, [], T.oc[:], qx[:].bitcast(dt.uint8))
-    dma("a", ["yb%d" % i for i in range(NR)], [], T.y[:], T.yb[:])
     for k, q in enumerate(SQ):
         dma(q, every, [], T.osc[4 * k:4 * k + 4, :], sx[32 * k:32 * k + 4, :])
+    dma("a", ["yb2", "yb1", "yb0"], [], T.y[:], T.yb[:])
+
+    count = {"v": 0, "a": 0, "p": 0, "g": 0}
+    waited, top, writer, readers, bank, ndma = {}, {}, {}, {}, {}, 0
+    for name, kind, q, rd, wr, call in arrange(steps):
+        need = [writer[k] for k in rd]
+        if kind != "send":
+            for k in wr:
+                need += readers.get(k, []) + ([writer[k]] if k in writer else [])
+        for k in rd + wr:
+            if k.startswith("ps"):
+                need += [tok for e, tok in bank.get(k, {}).items() if e != q]
+        for s in sorted(set(z for z, n in need)):
+            n = max(n for z, n in need if z == s)
+            if waited.get((q, s), 0) < n:
+                Q[q].wait_ge(T.sem[s], n)
+                waited[(q, s)] = n
+        if kind == "send":
+            for s, n, many in call():
+                top["sent"] = top.get("sent", 0) + n
+                top[s] = top.get(s, 0) + n * many
+                writer[s] = (s, top[s])
+            continue
+        if kind == "dma":
+            tok = ("d%d" % ndma, 16)
+            ndma += 1
+            call().then_inc(T.sem[tok[0]], 16)
+        else:
+            count[q] += 1
+            tok = ("e" + q, count[q])
+            call().then_inc(T.sem[tok[0]], 1)
+        top[tok[0]] = tok[1]
+        for k in rd:
+            readers.setdefault(k, []).append(tok)
+        for k in wr:
+            writer[k] = tok
+            readers[k] = []
+        for k in rd + wr:
+            if k.startswith("ps"):
+                bank.setdefault(k, {})[q] = tok
 
     for s in sorted(top):
         if max([n for (q, z), n in waited.items() if z == s] + [0]) < top[s]:
-            wait("g", (s, top[s]))
+            g.wait_ge(T.sem[s], top[s])

from concourse.bass import DstId, RemoteDMATransfer
from concourse.mybir import dt, AluOpType, AxisListType, ActivationFunctionType

C = 384
M = 64
ROUNDS = 2
MS = 400
BIG = -1.0e20
MAGIC = 3072
LIFT = 2048.0
TINY = 2.0 ** -120
RUNS = [(0, 128), (128, 256), (256, 384)]
MARK = [(0,), (1,), (2,)]
FL = 2 * C
PLACE = 160
PICK = [("a", 3, 0, 192), ("v", 0, 0, 192), ("a", 2, 0, C), ("v", 3, 192, C), ("a", 1, 0, C), ("v", 0, 192, C)]
CELL = "aaav"
RELU = "vava"
BACK = "vava"
FUSE = [(0, 2), (0, 2), (0, 2)]
SIDE = {0: 0, 2: 1, 1: 2, 3: 3}
SQ = "gssa"
ORDER = """
pidx.1 ut.1 st0_0.1 wf0z.1 jm.1 i31.1 i30.1 i32.1 wtz.1 row.1 st0_1.1 bits0.1 gam0.1 f3.1 ji.1 lt6.1 zhz.1 rh.1 st0_2.1 bits2.1 dbl.1 zi.1 c0.1 qu.1
wk.1 qx0_0.1 ni.1 bits1.1 low.1 wt0.1 zh.1 ps1.1 qx0_1.1 wt1.1 jb2.1 ps2.1 bits0.2 qw.1 qx0_2.1 c2.1 qk.1 vt.1 bits1.2 qb0.1 ps3.1 qq.1 nbm.1 sw.1
ps4.1 qb1.1 bits2.2 qj3.1 ps0.1 keyc.1 ps1.2 kb0.1 qb2.1 cs0.1 ps2.2 kq0.1 nbc.1 oh1_0.1 kb1.1 ps3.2 oh0_0.1 oh3_0.1 gam.1 ps4.2 oh2_0.1 kq1.1 ps7.1
kb2.1 oh1_1.1 oh3_1.1 pen0.1 oh2_1.1 oh0_1.1 kq2.1 jc.1 oh3_2.1 bs.1 oh2_2.1 oh0_2.1 oh1_2.1 qf.1 cs.1 pen1.1 spare.1 bh.1 num.1 ql.1 pent0.1 pent1.1
vv1.1 em.1 vv0.1 neg.1 mxz.1 atz.1 vtr1.1 vtr0.1 flag0.1 ms1.1 ms0.1 qj2.1 pb0.1 zt.1 emd.1 ps5.1 pd0.1 qj0.1 pl0.1 qj1.1 dh3.1 ps0.2 wf0.1 dh2.1
ps6.1 stf.1 enf.1 bh2.1 dh0.1 wtr0.1 wtr1.1 dh1.1 srcf0.1 fl.1 el.1 srcf1.1 sl0.1 ff0.1 sl1.1 ds0.1 ds1.1 ds3.1 ds4.1 ds5.1 ds2.1 mx3.1 mx1.1 mx0.1
at1.1 mx2.1 at0.1 at3.1 qe0.1 at2.1 c1_0.1 c1_256.1 qa0.1 qe1.1 c1_128.1 offc0.1 lift.1 nb.1 klf.1 ks.1 gtz.1 qe2.1 qe3.1 klf.2 na.1 nc.1 offs0.1
kl3_1_0.1 kl3_1_1.1 kl3_0_1.1 wf1z.1 kl3_2_0.1 ps7.2 ps5.2 fth0.1 ps6.2 fth0.2 ps4.3 acc0_1.1 acc0_3.1 ps1.3 kl3_2_1.1 acc1_1.1 ps0.3 acc0_0.1
acc1_3.1 acc0_2.1 ps3.3 kl3_0_0.1 wf1z.2 acc1_0.1 ps2.3 acc1_2.1 acc2_1.1 ps5.3 acc2_0.1 ztz.1 acc2_3.1 ps4.4 acc2_2.1 acc3_1.1 acc3_0.1 flag1.1 ps6.3
acc3_2.1 acc3_3.1 ps7.3 wf1z.3 acc4_0.1 acc4_1.1 ps1.4 acc4_2.1 ps0.4 acc4_3.1 acc5_0.1 acc5_1.1 ps2.4 acc5_2.1 acc5_3.1 ps3.4 acc6_0.1 acc6_1.1
acc6_2.1 ps7.4 acc6_3.1 zt_0.1 zt_1.1 zt_2.1 zt_3.1 keyl.1 qz0.1 ps2.5 ps3.5 ps0.5 gt2_0.1 ps1.5 gt3_0.1 gt0_0.1 gt1_0.1 qh0.1 qv.1 ps4.5 ps1.6 ps0.6
dg0.1 ps2.6 dg2.1 st1_0_0.1 ps6.4 dg1.1 dg3.1 st1_0_2.1 gb0.1 gb2.1 st1_0_3.1 st1_0_1.1 gb1.1 st1_2_1.1 st1_2_3.1 qx1_0.1 st1_1_1.1 st1_1_3.1 ps1.7
qx1_2.1 qx1_1.1 bits0.3 ps3.6 ps2.7 qb0.2 bits2.3 bits1.3 ps4.6 qb2.2 ps0.7 qb1.2 kb0.2 ps3.7 kq0.2 ps2.8 oh1_0.2 ps1.8 kb2.2 oh0_0.2 oh2_0.2 flag1.2
ps4.7 oh3_0.2 kq1.2 ps0.8 oh1_2.2 kb1.2 oh2_2.2 kq2.2 pen1.2 oh3_2.2 pen0.2 oh0_2.2 oh2_1.2 ps5.4 oh1_1.2 qf.2 bs.2 oh0_1.2 oh3_1.2 ql.2 ps6.5 cs.2
bh.2 ps7.5 pent0.2 vv0.2 vv1.2 em.2 pent1.2 bh2.2 vtr0.2 dh2.2 vtr1.2 ms0.2 ms1.2 dh1.2 pb0.2 emd.2 nb.2 dh0.2 pd0.2 stf.2 pl0.2 fl.2 enf.2 dh3.2
wf1.1 wtr1.2 wtr0.2 srcf1.2 srcf0.2 el.2 sl1.2 sl0.2 ff1.1 ds3.2 ds2.2 ds5.2 ds0.2 ds1.2 mx2.2 ds4.2 mx3.2 mx0.2 at2.2 mx1.2 at0.2 at3.2 at1.2 klf.3
qa1.1 ks.2 offc1.1 klf.4 offs1.1 na.2 nc.2 ps5.5 kl3_2_1.2 kl3_1_1.2 ps6.6 kl3_0_0.2 kl3_1_0.2 kl3_0_1.2 fth1.1 ps7.6 acc0_1.2 fth1.2 ps4.8 acc0_2.2
ps2.9 acc1_2.2 ps1.9 acc0_0.2 acc1_1.2 acc0_3.2 ps3.8 kl3_2_0.2 acc1_0.2 ps0.9 acc1_3.2 acc2_2.2 ps6.7 acc2_1.2 acc2_3.2 ps5.6 acc2_0.2 keyl.2
acc3_1.2 ps7.7 acc3_2.2 acc3_3.2 ps4.9 acc3_0.2 acc4_1.2 ps2.10 acc4_2.2 acc4_3.2 ps1.10 acc4_0.2 acc5_1.2 acc5_2.2 ps3.9 acc5_3.2 acc5_0.2 ps0.10
acc6_1.2 acc6_2.2 ps7.8 acc6_3.2 acc6_0.2 zt_1.2 zt_2.2 zt_3.2 zt_0.2 ps6.8 qz1.1 ps2.11 ps3.10 ps0.11 gt2_0.2 ps1.11 gt3_0.2 gt0_0.2 gt1_0.2 qh1.1
ps1.12 ps4.10 ps0.12 dg2.2 ps2.12 dg0.2 st2_0_2.1 dg1.2 dg3.2 st2_0_0.1 gb0.2 gb1.2 st2_0_1.1 st2_0_3.1 gb2.2 st2_1_3.1 st2_1_1.1 qx2_0.1 st2_2_3.1
st2_2_1.1 ps1.13 qx2_1.1 qx2_2.1 yb0.1 ps2.13 qx2_0.2 qx2_0.3 ps3.11 yb1.1 yb2.1 qx2_0.4 yb2.2 qx2_0.5 qx2_0.6
"""
CODE, U8, BF, F32, I32, U16 = "float8_e4m3fn_x4", "uint8", "bfloat16", "float32", "int32", "uint16"

SCRATCH = {"ps%d" % _b: ("psum", [128, 512], F32) for _b in range(8)}
for _n, _w, _d in [
        ("st0", 4 * C, BF), ("st1", 4 * C, BF), ("st2", 4 * C, BF), ("ut", 512, BF), ("vt", 512, BF),
        ("qu", 128, CODE), ("su", 128, U8), ("qv", 128, CODE), ("sv", 128, U8), ("qw", 512, CODE), ("sw", 512, U8),
        ("pidx", 4, I32), ("i3", 4, I32), ("f3", 4, F32), ("row", 24, F32), ("dbl", 16, F32), ("cst", 16, F32),
        ("keyc", 4, BF), ("spare", 4, F32), ("jc", 24, F32), ("gam0", 24, F32), ("gam", 24, F32),
        ("zi", 128, BF), ("zt", 520, BF), ("zh", 520, BF), ("ji", 128, BF), ("wt", 520, BF),
        ("qe", 512, CODE), ("se", 512, U8), ("qj", 512, CODE), ("sj", 512, U8), ("qk", 256, CODE), ("sk", 256, U8),
        ("jm", 128, BF), ("c0", 128, BF), ("c1", C, BF), ("c2", 128, BF), ("ni", C, BF), ("num", C + M, BF),
        ("bits", 4 * C, BF), ("qb", C, CODE), ("sb", C, U8), ("dh", 4 * C, BF), ("kb", C, BF), ("junk", C, BF),
        ("bsum", 8, F32), ("pen", C, BF), ("pent", C, BF), ("klf", C, F32), ("oh", 4 * C, BF), ("cs", 16 + 4 * C, BF),
        ("ks", C, F32), ("kq", C, BF),
        ("qf", 24, F32), ("ql", 24, U16), ("na", 24, F32), ("nb", 24, F32), ("nc", 96, F32), ("keyl", 96, U16),
        ("vv", C, BF), ("vtr", C, BF), ("ms", C, BF), ("pb", 24, BF), ("pd", 24, F32), ("pl", 24, U16), ("fl", 4, U16),
        ("wf0", FL, BF), ("wf1", FL, BF), ("ff0", 848, BF), ("ff1", 848, BF), ("wtr", 2 * C, BF), ("srcf", 24, F32), ("sl", 24, U16),
        ("em", 4, F32), ("emd", 4, F32), ("stf", 4, F32), ("enf", 4, F32), ("el", 4, U16),
        ("ds", 4 * C, BF), ("mx", 4 * MS, BF), ("at", 512, BF),
        ("acc", 8 * 4 * M, BF), ("ztile", 512, BF), ("gtile", 512, BF), ("dg", 4 * M, BF), ("gb", 3 * C, BF),
        ("yb", C, F32)]:
    SCRATCH[_n] = ("sbuf", [128, _w], _d)
for _t in range(ROUNDS + 1):
    SCRATCH["qx%d" % _t] = ("sbuf", [128, C], CODE)
    SCRATCH["sx%d" % _t] = ("sbuf", [128, C], U8)
for _t in range(ROUNDS):
    for _n, _w in (("a", 5 * M), ("c", 4 * M), ("z", 128), ("h", 128)):
        SCRATCH["q%s%d" % (_n, _t)] = ("sbuf", [128, _w], CODE)
        SCRATCH["s%s%d" % (_n, _t)] = ("sbuf", [128, _w], U8)

SEMAPHORES = (["ev", "ea", "ep", "eg", "sent"]
              + [_n + str(_t) for _n in ("sibc", "sibs", "offc", "offs", "fwd", "fth") for _t in range(ROUNDS)]
              + ["d%d" % i for i in range(24)])


def arrange(steps):
    if not ORDER:
        return steps
    at = {n: i for i, n in enumerate(ORDER.split())}
    return sorted(steps, key=lambda s: at[s[0]])


def rank_program(g, core, T, topo):
    rank = T.rank_of(core)
    if rank is None:
        return
    op, act = AluOpType, ActivationFunctionType
    Q = {"v": g.vector, "a": g.scalar, "p": g.tensor, "g": g, "s": g.sync}
    steps, seen = [], {}

    def step(kind, q, rd, wr, call):
        k = (list(wr) + list(rd))[0]
        seen[k] = seen.get(k, 0) + 1
        steps.append(("%s.%d" % (k, seen[k]), kind, q, list(rd), list(wr), call))

    def run(q, rd, wr, call):
        step("run", q, rd, wr, call)

    def dma(q, rd, wr, out, in_):
        step("dma", q, rd, wr, lambda: Q[q].dma_start(out, in_))

    def ts(rd, wr, out, in0, s1, s2, o0, o1=None):
        if o1 is None:
            run("v", rd, wr, lambda: g.vector.tensor_scalar(out, in0, s1, None, o0))
        else:
            run("v", rd, wr, lambda: g.vector.tensor_scalar(out, in0, s1, s2, o0, o1))

    def tt(rd, wr, out, a, b, o):
        run("v", rd, wr, lambda: g.vector.tensor_tensor(out, a, b, o))

    def cp(rd, wr, out, in_):
        run("v", rd, wr, lambda: g.vector.tensor_copy(out, in_))

    def fill(wr, ap, c):
        run("v", [], wr, lambda: g.vector.memset(ap, c))

    def scan(rd, wr, out, d0, d1, init, o0, o1):
        run("v", rd, wr, lambda: g.vector.tensor_tensor_scan(out, d0, d1, init, o0, o1))

    def turn(rd, wr, out, in_):
        run("v", rd, wr, lambda: g.vector.transpose(out, in_))

    def quant(rd, wr, qo, so, in_):
        run("v", rd, wr, lambda: g.vector.quantize_mx(qo, so, in_))

    def av(rd, wr, out, in_, func, **kw):
        run("a", rd, wr, lambda: g.scalar.activation(out, in_, func, **kw))

    def move(q, rd, wr, out, in_):
        if q == "a":
            av(rd, wr, out, in_, act.Copy)
        else:
            cp(rd, wr, out, in_)

    def mm(rd, b, n, lq, ls, rq, rs):
        run("p", rd, ["ps%d" % b], lambda: g.tensor.matmul_mx(T["ps%d" % b][:, 0:n], lq, ls, rq, rs, True, True))

    def iota(wr, out, pat, base, cm, small=True):
        if small:
            run("g", [], wr, lambda: g.iota(out, pat, base, cm, allow_small_or_imprecise_dtypes=True))
        else:
            run("g", [], wr, lambda: g.iota(out, pat, base, cm))

    def ps(b, a, z):
        return T["ps%d" % b][:, a:z]

    def whole(rd, bk, b, n, rq, rs):
        mm(rd + ["qe%d" % b], bk, n, T.qe[:, 128 * b:128 * b + 128], T.se[:, 128 * b:128 * b + 128], rq, rs)

    def halved(rd, bk, b, n, rq, rs):
        mm(rd + ["qj%d" % b], bk, n, T.qj[:, 128 * b:128 * b + 128], T.sj[:, 128 * b:128 * b + 128], rq, rs)

    others = [c for c in T.cores if c != core]
    sib = [c for c in others if c in topo.cores_of(core)][0]
    far = [c for c in others if c not in topo.cores_of(core) and topo.die(c) == topo.die(core)]
    mate = [c for c in far if topo.mates(core, c)][0]
    across = [c for c in far if topo.same_plane(core, c)][0]
    fourth = [c for c in far if c != mate and c != across][0]
    off_mask = topo.mask(core, mate) & topo.mask(core, across) & topo.mask(core, fourth)
    on_mask = topo.mask(core, sib) & ~off_mask

    def dst(c):
        rid, pid = topo.addr(c, core)
        return DstId(rid=rid, pnc=pid)

    def send(rd, trs):
        def call():
            g.remote_dma_fused([RemoteDMATransfer(dst_ids=[dst(c) for c in cs], dma_engine_mask=m, remote_sem=T.sem[s], src=src, dsts=ds)
                                for cs, m, s, src, ds in trs], local_sem=T.sem.sent)
            return [(s, bin(m).count("1"), len(cs)) for cs, m, s, src, ds in trs]
        step("send", "g", rd, [tr[2] for tr in trs], call)

    NR = len(RUNS)
    L = NR - 1
    dma("a", [], ["ut"], T.ut[:], T.u[:])
    for i, (lo, hi) in enumerate(RUNS):
        dma("s", [], ["st0_%d" % i], T.st0[:, 4 * lo:4 * hi], T.x[:, 4 * lo:4 * hi])
    dma("s", ["st0_%d" % L], ["qw"], T.qw[:].bitcast(dt.uint8), T.wc[:])
    dma("s", ["st0_%d" % L], ["sw"], T.sw[:], T.ws[:])
    dma("g", ["st0_%d" % L], ["vt"], T.vt[:], T.v[:])

    iota(["pidx"], T.pidx[:, 0:1], [[0, 1]], 0, 4, False)
    iota(["row"], T.row[:], [[1, 24]], 0, 0)
    iota(["ji"], T.ji[:], [[1, 8], [0, 16]], 0, 0)
    iota(["jm"], T.jm[:], [[0, 8], [1, 16]], 0, 0)
    iota(["zi"], T.zi[:], [[1, 128]], 0, -1)
    iota(["gam0"], T.gam0[:], [[0, 12], [16, 2]], MAGIC + 183, 0)
    iota(["ni"], T.ni[:], [[32, 12], [0, 2], [1, 16]], -192, 0)

    fill(["wf0z"], T.wf0[:], 0.0)
    for i, (lo, hi) in enumerate(RUNS):
        av(["wf0z"], ["bits%d" % i], T.bits[:, 4 * lo:4 * hi], T.wf0[:, 0:4 * (hi - lo)], act.Copy)
    ts(["pidx"], ["i30"], T.i3[:, 0:1], T.pidx[:, 0:1], 2, 15, op.arith_shift_right, op.bitwise_and)
    ts(["pidx"], ["i31"], T.i3[:, 1:2], T.pidx[:, 0:1], 6, None, op.arith_shift_right)
    ts(["pidx"], ["i32"], T.i3[:, 2:3], T.pidx[:, 0:1], 2, 16, op.arith_shift_right, op.bitwise_and)
    fill(["wtz"], T.wt[:], 0.0)
    cp(["i30", "i31", "i32"], ["f3"], T.f3[:, 0:3], T.i3[:, 0:3])
    r, grp, par16 = T.f3[:, 0:1], T.f3[:, 1:2], T.f3[:, 2:3]
    fill(["zhz"], T.zh[:], 0.0)
    wk, lift, nb, rh, nm, low, wq = [T.cst[:, i:i + 1] for i in range(7)]
    ts(["row", "f3"], ["dbl"], T.dbl[:, 0:15], T.row[:, 0:15], r, 1.0, op.is_lt, op.add)
    ts(["f3"], ["lt6"], T.dbl[:, 15:16], r, 6.0, 0.5, op.is_lt, op.mult)
    ts(["f3"], ["low"], low, r, 2.0, 1.0, op.is_lt, op.mult)
    ts(["zi", "zhz"], ["zh"], T.zh[:, 3:515:4], T.zi[:], 0.0, 0.5, op.is_equal, op.mult)
    run("v", ["dbl", "lt6"], ["wk"], lambda: g.vector.tensor_reduce(wk, T.dbl[:], AxisListType.X, op.mult))
    ts(["jm", "f3"], ["c0"], T.c0[:], T.jm[:], r, -32.0 * LIFT, op.is_equal, op.mult)
    ts(["ji", "f3", "wk", "wtz"], ["wt0"], T.wt[:, 0:512:4], T.ji[:], grp, wk, op.is_equal, op.mult)
    ts(["wt0", "low"], ["wt1"], T.wt[:, 1:512:4], T.wt[:, 0:512:4], low, None, op.mult)
    quant(["wt0", "wt1"], ["qk"], T.qk[:, 0:128], T.sk[:, 0:128], T.wt[:, 0:512])
    quant(["wt0", "wt1"], ["qq"], T.qk[:, 128:256], T.sk[:, 128:256], T.wt[:, 1:513])
    quant(["ut"], ["qu"], T.qu[:], T.su[:], T.ut[:])
    av(["f3"], ["rh"], rh, r, act.Identity, scale=4.0, bias=0.5)
    av(["f3"], ["nbc"], nb, r, act.Identity, scale=8192.0)
    av(["f3"], ["nbm"], nm, r, act.Identity, scale=-8192.0)
    av(["f3"], ["lift"], lift, r, act.Identity, scale=LIFT / 4 + 63.0, bias=23.5 - 15.0 * (LIFT / 4 + 63.0))
    av(["f3"], ["jb2"], wq, r, act.Identity, scale=4.0 + 1.0 / C, bias=1.5 - 60.0)
    av(["c0"], ["c2"], T.c2[:], T.c0[:], act.Identity, scale=4.0 / LIFT, bias=4.0)
    av(["gam0"], ["gam"], T.gam[:], T.gam0[:], act.Identity, bias=0.5)
    av(["row", "rh"], ["keyc"], T.keyc[:], T.row[:, 0:4], act.Identity, bias=rh)
    av(["row", "jb2"], ["jc"], T.jc[:], T.row[:], act.Identity, scale=16.0 / C, bias=wq)
    for a in range(0, C, 128):
        av(["c0"], ["c1_%d" % a], T.c1[:, a:a + 128], T.c0[:], act.Identity, bias=LIFT)
    av(["keyc"], ["spare"], T.spare[:], T.keyc[:], act.Identity, bias=384.5)
    for b in range(4):
        quant(["zh"], ["qj%d" % b], T.qj[:, 128 * b:128 * b + 128], T.sj[:, 128 * b:128 * b + 128], T.zh[:, 3 - b:515 - b])
    av(["wf0z"], ["neg"], T.num[:, C:C + M], T.wf0[:, 0:M], act.Identity, bias=BIG)
    av(["wf0z"], ["mxz"], T.mx[:, C:4 * MS:MS], T.wf0[:, 0:4], act.Copy)
    av(["wf0z"], ["cs0"], T.cs[:, 15:16], T.wf0[:, 0:1], act.Identity, bias=-192.0)
    av(["ni", "f3"], ["num"], T.num[:, 0:C], T.ni[:], act.Identity, bias=par16)
    av(["wf0z"], ["atz"], T.at[:, 0:256], T.wf0[:, 0:256], act.Copy)
    av(["wf0z"], ["flag0"], T.ff0[:, 0:C], T.wf0[:, 0:C], act.Copy)

    HB = {2: 5, 1: 6, 3: 7}
    FREE = 8
    PB, KB, QB = [1, 2, 3], [4, 1, 3], [0, 2, 4]
    apart = [[b for b in (2, 1, 3) if b not in FUSE[i]] for i in range(NR)]
    first = [0 if 2 in apart[i] else 2 for i in range(NR)]
    at = [24 + sum(len(apart[j]) * (RUNS[j][1] - RUNS[j][0]) // 16 for j in range(i)) for i in range(NR + 1)]

    def state(t):
        st = T["st%d" % t]
        for i, (lo, hi) in enumerate(RUNS):
            n = len(apart[i]) * (hi - lo)
            av(["dg0", "dg2"] * (first[i] == 0) + ["dg1", "dg3", "keyl"], ["gb%d" % i],
               T.gb[:, 3 * lo:3 * lo + n], T.dg[:, M * first[i]:4 * M].indirect(T.keyl[:, at[i]:at[i + 1]]), act.Copy)
        for b in range(4):
            rs = [i for i in range(NR) if b in FUSE[i]]
            if rs:
                lo, hi = RUNS[rs[0]][0], RUNS[rs[-1]][1]
                tt(["dg%d" % b, "keyl", "dh%d" % b], ["st%d_%d_%d" % (t, i, b) for i in rs], st[:, 4 * lo + b:4 * hi:4],
                   T.dg[:, M * SIDE[b]:M * SIDE[b] + M].indirect(T.keyl[:, lo // 16:hi // 16]), T.dh[:, C * b + lo:C * b + hi], op.add)
        for i, (lo, hi) in enumerate(RUNS):
            for k, b in enumerate(apart[i]):
                a = 3 * lo + k * (hi - lo)
                tt(["ps%d" % HB[b], "gb%d" % i], ["st%d_%d_%d" % (t, i, b)], st[:, 4 * lo + b:4 * hi:4], ps(HB[b], lo, hi),
                   T.gb[:, a:a + hi - lo], op.add)
            quant_run(t, i)

    def quant_run(t, i):
        lo, hi = RUNS[i]
        rd = ["st%d_%d_%d" % (t, i, b) for b in range(4)] if t else ["st0_%d" % i]
        quant(rd, ["qx%d_%d" % (t, i)], T["qx%d" % t][:, lo:hi], T["sx%d" % t][:, lo:hi], T["st%d" % t][:, 4 * lo:4 * hi])

    for t in range(ROUNDS):
        qx, sx = T["qx%d" % t], T["sx%d" % t]
        qa, sa, qc, sc = T["qa%d" % t], T["sa%d" % t], T["qc%d" % t], T["sc%d" % t]
        qz, sz, qh, sh = T["qz%d" % t], T["sz%d" % t], T["qh%d" % t], T["sh%d" % t]
        wf, ff = T["wf%d" % t], T["ff%d" % t]
        kw, kf = "wf%d" % t, "ff%d" % t
        kx = ["qx%d_%d" % (t, i) for i in range(NR)]

        if t:
            state(t)
        else:
            for i in range(NR):
                quant_run(t, i)
        for i, (lo, hi) in enumerate(RUNS):
            mm(["qu", kx[i]], PB[i], hi - lo, T.qu[:], T.su[:], qx[:, lo:hi], sx[:, lo:hi])
            av(["ps%d" % PB[i]], ["bits%d" % i], T.bits[:, 4 * lo:4 * hi:4], ps(PB[i], 0, hi - lo), act.Sign, bias=-TINY)
        for i, (lo, hi) in enumerate(RUNS):
            n = hi - lo
            quant(["bits%d" % i], ["qb%d" % i], T.qb[:, lo:hi], T.sb[:, lo:hi], T.bits[:, 4 * lo:4 * hi])
            mm(["qk", "qb%d" % i], KB[i], n, T.qk[:, 0:128], T.sk[:, 0:128], T.qb[:, lo:hi], T.sb[:, lo:hi])
            mm(["qq", "qb%d" % i], QB[i], n, T.qk[:, 128:256], T.sk[:, 128:256], T.qb[:, lo:hi], T.sb[:, lo:hi])
            av(["ps%d" % KB[i]], ["kb%d" % i], T.kb[:, lo:hi], ps(KB[i], 0, n), act.Identity, bias=32.0)
            scan(["c2", "ps%d" % QB[i]], ["kq%d" % i], T.kq[:, lo:hi], T.c2[:, 0:n], ps(QB[i], 0, n), 0.0, op.add, op.max)
        for rs in MARK:
            lo, hi = RUNS[rs[0]][0], RUNS[rs[-1]][1]
            for q in range(4):
                ts(["kb%d" % i for i in rs] + ["keyc"], ["oh%d_%d" % (q, i) for i in rs], T.oh[:, C * q + lo:C * q + hi], T.kb[:, lo:hi],
                   T.keyc[:, q:q + 1], 0.5, op.is_equal, op.mult)
        kbk, kqk = ["kb%d" % i for i in range(NR)], ["kq%d" % i for i in range(NR)]
        tt(kqk + ["jc"], ["qf"], T.qf[:], T.kq[:, 15:C:16], T.jc[:], op.add)
        ts(["qf"], ["ql"], T.ql[:], T.qf[:], float(C), None, op.mult)
        bh, bh2 = T.bsum[:, 1:2], T.bsum[:, 2:3]
        av(kbk + ["nbc"], ["bs", "junk"], T.junk[:], T.kb[:], act.Sign, scale=-2048.0, bias=nb, accum_out=T.bsum[:, 0:1])
        av(["bs"], ["bh"], bh, T.bsum[:, 0:1], act.Identity, scale=0.5, bias=192.0)
        av(["bs"], ["bh2"], bh2, T.bsum[:, 0:1], act.Identity, scale=0.5, bias=383.0)
        cut = RUNS[L][0]
        for k, (lo, hi) in enumerate(((0, cut), (cut, C))):
            av((kbk[:L], kbk[L:])[k] + ["nbm"], ["pen%d" % k], T.pen[:, lo:hi], T.kb[:, lo:hi], act.Relu, scale=2048.0, bias=nm)
            turn(["pen%d" % k], ["pent%d" % k], T.pent[:, lo:hi], T.pen[:, lo:hi])
        for b, bk in ((1, HB[1]), (0, 0), (2, HB[2]), (3, HB[3])):
            halved(kx, bk, b, C, qx[:], sx[:])
            av(["ps%d" % bk], ["dh%d" % b], T.dh[:, C * b:C * b + C], ps(bk, 0, C), act.Copy)

        scan(["oh%d_%d" % (q, i) for q in range(4) for i in range(NR)], ["cs"], T.cs[:, 16:16 + 4 * C], T.oh[:], T.oh[:],
             -192.0, op.add, op.add)
        ends, starts = T.cs[:, 15 + C:16 + 4 * C:C], T.cs[:, 15:16 + 3 * C:C]
        win = T.cs[:, 16:16 + 4 * C]
        tt(["cs", "cs0"], ["em"], T.em[:], ends, starts, op.is_equal)
        ts(["cs", "ql", "bh"], ["vv0"], T.vv[:, 0:PLACE], win.indirect(T.ql[:, 0:PLACE // 16]), bh, None, op.add)
        av(["cs", "ql", "bh"], ["vv1"], T.vv[:, PLACE:C], win.indirect(T.ql[:, PLACE // 16:C // 16]), act.Identity, bias=bh)
        parts = [(0, PLACE), (PLACE, C)]
        tt(["em", "spare"], ["emd"], T.emd[:], T.em[:], T.spare[:], op.mult)
        for k, (lo, hi) in enumerate(parts):
            turn(["vv%d" % k], ["vtr%d" % k], T.vtr[:, lo:hi], T.vv[:, lo:hi])
        tt(["emd", "cs", "cs0"], ["stf"], T.stf[:], T.emd[:], starts, op.add)
        for k, (lo, hi) in enumerate(parts):
            scan(["pent0"] * (lo < cut) + ["pent1"] * (hi > cut) + ["vtr%d" % k], ["ms%d" % k], T.ms[:, lo:hi], T.pent[:, lo:hi],
                 T.vtr[:, lo:hi], 0.0, op.add, op.min)
        km = ["ms0", "ms1"]
        ts(["stf", "bh"], ["fl"], T.fl[:], T.stf[:], bh, 192.0, op.add, op.add)
        tt(km + ["gam"], ["pb0"], T.pb[:], T.ms[:, 15:C:16], T.gam[:], op.add)
        tt(["pb0"] + km, ["pd0"], T.pd[:], T.pb[:], T.ms[:, 15:C:16], op.add)
        ts(["pd0"], ["pl0"], T.pl[:], T.pd[:], 191.0 - MAGIC, None, op.add)
        cp(["pl0", "num"], [kw, "wf%dz" % t], wf[:].indirect(T.pl[:]), T.num[:, 0:C])
        tt(["emd", "cs"], ["enf"], T.enf[:], T.emd[:], ends, op.add)
        ts(["enf", "bh2"], ["el"], T.el[:], T.enf[:], bh2, float(C), op.add, op.min)
        av(kbk, ["klf"], T.klf[:], T.kb[:], act.Identity, bias=-0.5)
        dma("s", ["klf"], [], T.kl[8 * t:8 * t + 8, :], T.klf[0:128:16, :])
        cp(["fl", "neg", "flag%d" % t], [kf], ff[:].indirect(T.fl[:]), T.num[:, C:C + M])
        twos = [(0, C // 2), (C // 2, C)]
        for k, (lo, hi) in enumerate(twos):
            a, z = lo // 16, hi // 16
            turn([kw], ["wtr%d" % k], T.wtr[:, 2 * lo:2 * hi], wf[:, 2 * lo:2 * hi])
            tt(["wtr%d" % k], ["srcf%d" % k], T.srcf[:, a:z], T.wtr[:, 2 * lo:2 * hi:32], T.wtr[:, 2 * lo + 16:2 * hi:32], op.add)
            ts(["srcf%d" % k], ["sl%d" % k], T.sl[:, a:z], T.srcf[:, a:z], 192.0, None, op.add)

        for k, (q, b, lo, hi) in enumerate(PICK):
            move(q, ["dh%d" % b] + ["sl%d" % j for j, (a, z) in enumerate(twos) if a < hi and lo < z], ["ds%d" % k],
                 T.ds[:, C * b + lo:C * b + hi], T.dh[:, C * b:C * b + C].indirect(T.sl[:, lo // 16:hi // 16]))
        for b in range(4):
            scan([kf] + ["ds%d" % k for k in range(len(PICK)) if PICK[k][1] == b], ["mx%d" % b], T.mx[:, MS * b:MS * b + C],
                 ff[:, 0:C], T.ds[:, C * b:C * b + C], 0.0, op.add, op.max)
        for b, q in enumerate(CELL):
            src, out = T.mx[:, MS * b:MS * b + C + 1].indirect(T.el[:]), T.at[:, 256 + b:512:4]
            if q == "a":
                av(["mx%d" % b, "mxz", "el"], ["at%d" % b], out, src, act.Copy, scale=2.0)
            else:
                ts(["mx%d" % b, "mxz", "el"], ["at%d" % b], out, src, 2.0, None, op.mult)
        ka = "qa%d" % t
        quant(["at0", "at1", "at2", "at3", "atz"], [ka], qa[:, 0:128], sa[:, 0:128], T.at[:])

        def vx(bb, z, a, e):
            return bb[:, a:e].bitcast(dt.uint8) if z == "c" else bb[:, a:e]
        sfx = str(t)
        both = ((qa, qc, "c"), (sa, sc, "s"))
        for buf, lnd, z in both:
            send([ka], [([mate, across], off_mask, "off" + z + sfx, vx(buf, z, M, 2 * M), [vx(buf, z, 3 * M, 4 * M), vx(buf, z, 4 * M, 5 * M)]),
                        ([sib], on_mask, "sib" + z + sfx, vx(buf, z, M, 2 * M), [vx(buf, z, 2 * M, 3 * M)])])
        for buf, lnd, z in both:
            send(["sib" + z + sfx, "off" + z + sfx],
                 [([fourth], off_mask, "fth" + sfx, vx(buf, z, M, 3 * M), [vx(lnd, z, 2 * M, 4 * M)]),
                  ([sib], on_mask, "fwd" + sfx, vx(buf, z, 3 * M, 5 * M), [vx(lnd, z, 0, 2 * M)])])

        if t == 0:
            av(["zh"], ["zt"], T.zt[:], T.zh[:], act.Copy, scale=2.0)
            for b in range(4):
                quant(["zt"], ["qe%d" % b], T.qe[:, 128 * b:128 * b + 128], T.se[:, 128 * b:128 * b + 128], T.zt[:, 3 - b:515 - b])
        scan(["c1_%d" % a for a in range(0, C, 128)] + kbk, ["ks"], T.ks[:], T.c1[:], T.kb[:], 0.0, op.add, op.max)
        av(["ks", "lift"], ["na"], T.na[:], T.ks[:, 15:C:16], act.Identity, scale=0.25, bias=lift)
        av(kqk, ["nb"], T.nb[:], T.kq[:, 15:C:16], act.Identity, scale=15.75)
        tt(["na", "nb"], ["nc"], T.nc[:, 0:24], T.na[:], T.nb[:], op.add)
        for i, (lo, hi) in enumerate(RUNS):
            n = (hi - lo) // 16
            for k, b in enumerate(apart[i]):
                a = at[i] + n * k
                av(["nc"], ["kl3_%d_%d" % (i, k)], T.nc[:, a:a + n], T.nc[:, lo // 16:hi // 16], act.Identity,
                   bias=float(M * (SIDE[b] - first[i])))
        cp(["nc"] + ["kl3_%d_%d" % (i, k) for i in range(NR) for k in range(len(apart[i]))], ["keyl"], T.keyl[:, 0:at[NR]], T.nc[:, 0:at[NR]])
        if t == 0:
            av(["atz"], ["ztz"], T.ztile[:, 256:512], T.at[:, 0:256], act.Copy)
            for a in range(0, FL, 256):
                av(["atz"], ["wf1z"], T.wf1[:, a:a + 256], T.at[:, 0:256], act.Copy)
            for a in range(0, C, 192):
                av(["atz"], ["flag1"], T.ff1[:, a:a + 192], T.at[:, 0:192], act.Copy)
            quant(["vt"], ["qv"], T.qv[:], T.sv[:], T.vt[:])

        def slot(i, b):
            return T.acc[:, (4 * i + b) * M:(4 * i + b + 1) * M]

        def batch(i, rd, rq, rs):
            bk = [(2 * i + b + 4) % FREE for b in range(4)]
            for b in range(4):
                whole(rd, bk[b], b, 2 * M, rq, rs)
                if i == 0:
                    av(["ps%d" % bk[b]], ["acc0_%d" % b], slot(0, b), ps(bk[b], 0, M), act.Copy)
                for j in range(max(i, 1), i + 2):
                    out, ko = (slot(j, b), "acc%d_%d" % (j, b)) if j < 7 else (T.ztile[:, b:256:4], "zt_%d" % b)
                    tt(["ps%d" % bk[b], "acc%d_%d" % (j - 1, b)], [ko], out, ps(bk[b], M * (j - i), M * (j - i) + M), slot(j - 1, b), op.max)
        batch(0, [ka, "sibc" + sfx, "sibs" + sfx], qa[:, M:3 * M], sa[:, M:3 * M])
        batch(2, ["offc" + sfx, "offs" + sfx], qa[:, 3 * M:5 * M], sa[:, 3 * M:5 * M])
        batch(4, ["fwd" + sfx], qc[:, 0:2 * M], sc[:, 0:2 * M])
        batch(6, ["fth" + sfx], qc[:, 2 * M:4 * M], sc[:, 2 * M:4 * M])
        for b in sorted(set(sum(apart, []))):
            halved(kx, HB[b], b, C, qx[:], sx[:])

        kz, kh = "qz%d" % t, "qh%d" % t
        quant(["zt_0", "zt_1", "zt_2", "zt_3", "ztz"], [kz], qz[:], sz[:], T.ztile[:])
        for b in range(4):
            mm([kz, "qw", "sw"], b, 128, T.qw[:, 128 * b:128 * b + 128], T.sw[:, 128 * b:128 * b + 128], qz[:], sz[:])
        if t == 0:
            av(["atz"], ["gtz"], T.gtile[:, 256:512], T.at[:, 0:256], act.Copy)
        for b in range(4):
            if RELU[b] == "a":
                av(["ps%d" % b], ["gt%d_0" % b], T.gtile[:, b:256:4], ps(b, 0, M), act.Relu, scale=0.015625)
            else:
                ts(["ps%d" % b], ["gt%d_0" % b], T.gtile[:, b:256:4], ps(b, 0, M), 0.0, 0.015625, op.max, op.mult)
        quant(["gt%d_0" % b for b in range(4)] + ["gtz"], [kh], qh[:], sh[:], T.gtile[:])
        for b, bk in enumerate((4, 0, 1, 2)):
            halved([kh], bk, b, 128, qh[:], sh[:])
            move(BACK[b], ["ps%d" % bk], ["dg%d" % b], T.dg[:, M * SIDE[b]:M * SIDE[b] + M], ps(bk, 0, M))

    t = ROUNDS
    qx, sx = T["qx%d" % t], T["sx%d" % t]
    every = ["qx%d_%d" % (t, i) for i in range(NR)]
    state(t)
    for i, (lo, hi) in enumerate(RUNS):
        mm([every[i], "qv"], 1 + i, hi - lo, T.qv[:], T.sv[:], qx[:, lo:hi], sx[:, lo:hi])
        move("a" if i < L else "v", ["ps%d" % (1 + i)], ["yb%d" % i], T.yb[:, lo:hi], ps(1 + i, 0, hi - lo))
    dma("s", every, [], T.oc[:], qx[:].bitcast(dt.uint8))
    for k, q in enumerate(SQ):
        dma(q, every, [], T.osc[4 * k:4 * k + 4, :], sx[32 * k:32 * k + 4, :])
    dma("a", ["yb2", "yb1", "yb0"], [], T.y[:], T.yb[:])

    count = {"v": 0, "a": 0, "p": 0, "g": 0}
    waited, top, writer, readers, bank, ndma = {}, {}, {}, {}, {}, 0
    for name, kind, q, rd, wr, call in arrange(steps):
        need = [writer[k] for k in rd]
        if kind != "send":
            for k in wr:
                need += readers.get(k, []) + ([writer[k]] if k in writer else [])
        for k in rd + wr:
            if k.startswith("ps"):
                need += [tok for e, tok in bank.get(k, {}).items() if e != q]
        for s in sorted(set(z for z, n in need)):
            n = max(n for z, n in need if z == s)
            if waited.get((q, s), 0) < n:
                Q[q].wait_ge(T.sem[s], n)
                waited[(q, s)] = n
        if kind == "send":
            for s, n, many in call():
                top["sent"] = top.get("sent", 0) + n
                top[s] = top.get(s, 0) + n * many
                writer[s] = (s, top[s])
            continue
        if kind == "dma":
            tok = ("d%d" % ndma, 16)
            ndma += 1
            call().then_inc(T.sem[tok[0]], 16)
        else:
            count[q] += 1
            tok = ("e" + q, count[q])
            call().then_inc(T.sem[tok[0]], 1)
        top[tok[0]] = tok[1]
        for k in rd:
            readers.setdefault(k, []).append(tok)
        for k in wr:
            writer[k] = tok
            readers[k] = []
        for k in rd + wr:
            if k.startswith("ps"):
                bank.setdefault(k, {})[q] = tok

    for s in sorted(top):
        if max([n for (q, z), n in waited.items() if z == s] + [0]) < top[s]:
            g.wait_ge(T.sem[s], top[s])
